import numpy as np
import ml_dtypes


def mxq(x, axis, fmt="e4m3"):
    dtype, down = {"e4m3": (ml_dtypes.float8_e4m3fn, 7), "e5m2": (ml_dtypes.float8_e5m2, 14)}[fmt]
    v = np.moveaxis(np.asarray(x, np.float32).astype(ml_dtypes.bfloat16).astype(np.float64), axis, -1)
    blocks = v.reshape(v.shape[:-1] + (-1, 32))
    amax = np.abs(blocks).max(-1, keepdims=True)
    byte = np.maximum(np.where(amax > 0, np.frexp(amax)[1] - 1 + 127, 0) - down, 1)
    scale = np.exp2(byte - 127.0)
    codes = (blocks / scale).astype(np.float32).astype(dtype).astype(np.float64)
    return np.moveaxis((codes * scale).reshape(v.shape), -1, axis)


WIDE = False


def mx_kscale(k):
    if not WIDE:
        return np.ones(k)
    levels = np.array([10, -10, 5, -5, 0])
    if k % 512:
        return np.exp2(np.random.permutation(np.resize(levels, k // 32))).repeat(32)
    a = np.empty((k // 512, 16))
    for p in range(k // 512):
        a[p, :8] = np.random.permutation(np.resize(levels, 8))
        for g in range(8):
            far = levels[np.abs(levels - a[p, g]) >= 10]
            a[p, g + 8] = far[np.random.randint(len(far))]
    return np.exp2(a.ravel()).repeat(32)


def f64(x):
    return np.asarray(x).astype(np.float64)


def striped(idx):
    return np.tile(idx.reshape(-1, 16).T, (8, 1)).astype(np.uint16)


def unstriped(offs):
    return offs[:16].T.reshape(-1).astype(np.int64)


def striped8(idx):
    return np.concatenate([x.reshape(-1, 16).T for x in idx]).astype(np.uint16)


def runs(offs, k):
    lists = np.stack([offs[16 * r : 16 * r + 16].T.reshape(-1) for r in range(8)]).astype(np.int64)
    return lists[np.arange(k) % 512 // 64]


def pack_weight(w):
    k, n = w.shape
    w = f64(np.asarray(w, np.float32).astype(ml_dtypes.bfloat16)).reshape(k // 32, 32, n)
    amax = np.abs(w).max(1)
    byte = np.clip(np.where(amax > 0, np.frexp(amax)[1] - 1 + 127 - 7, 1), 1, 254)
    scaled = (w * np.exp2(127.0 - byte)[:, None, :]).reshape(k, n).astype(np.float32)
    words = np.ascontiguousarray(scaled.reshape(k // 512, 128, 4, n).transpose(0, 1, 3, 2)).astype(ml_dtypes.float8_e4m3fn).view(np.uint8)
    return words, np.ascontiguousarray(byte.astype(np.uint8).reshape(k // 512, 16, n))


def unpack_weight(words, scales):
    g, p, n, _ = words.shape
    vals = np.ascontiguousarray(words).view(ml_dtypes.float8_e4m3fn).astype(np.float64) * np.repeat(np.exp2(scales.astype(np.float64) - 127.0), 8, axis=1)[..., None]
    return vals.transpose(0, 1, 3, 2).reshape(g * 512, n)


E2M1 = np.array([0.0, 0.5, 1.0, 1.5, 2.0, 3.0, 4.0, 6.0, -0.0, -0.5, -1.0, -1.5, -2.0, -3.0, -4.0, -6.0])


def pack_fp4(w):
    k, n = w.shape
    w = f64(np.asarray(w, np.float32).astype(ml_dtypes.bfloat16)).reshape(k // 32, 32, n)
    amax = np.abs(w).max(1)
    mant, ex = np.frexp(amax / 6.0)
    byte = np.clip(np.where(amax > 0, np.where(mant > 0.5, ex, ex - 1) + 127, 1), 1, 254)
    scaled = (w * np.exp2(127.0 - byte)[:, None, :]).reshape(k, n).astype(np.float32)
    c = np.ascontiguousarray(scaled.reshape(k // 512, 128, 4, n).transpose(0, 1, 3, 2)).astype(ml_dtypes.float4_e2m1fn).view(np.uint8) & 0xF
    words = (c[..., 0::2] | (c[..., 1::2] << 4)).reshape(k // 512, 128, 2 * n)
    return np.ascontiguousarray(words), np.ascontiguousarray(byte.astype(np.uint8).reshape(k // 512, 16, n))


def unpack_fp4(words, scales):
    g, _, n = scales.shape
    words = np.ascontiguousarray(words).reshape(g, 128, n, 2)
    nib = np.empty((g, 128, n, 4), np.uint8)
    nib[..., 0::2] = words & 0xF
    nib[..., 1::2] = words >> 4
    vals = E2M1[nib] * np.repeat(np.exp2(scales.astype(np.float64) - 127.0), 8, axis=1)[..., None]
    return vals.transpose(0, 1, 3, 2).reshape(g * 512, n)


def relu(v):
    return np.maximum(v, 0.0)

def planes(y):
    n, m = y.shape
    v = y.astype(np.float32).astype(ml_dtypes.bfloat16).astype(np.float64).reshape(n // 32, 32, m)
    top = np.abs(v).max(1)
    byte = np.clip(np.where(top > 0, np.frexp(top)[1] - 1 + 127 - 7, 1), 1, 254)
    codes = (v * np.exp2(127.0 - byte)[:, None, :]).reshape(n, m).astype(np.float32).astype(ml_dtypes.float8_e4m3fn).view(np.uint8)
    words = codes.reshape(n // 512, 128, 4, m).transpose(0, 1, 3, 2)
    return np.ascontiguousarray(words), np.ascontiguousarray(byte.astype(np.uint8).reshape(n // 512, 16, m))


K, T, S, N, H = 512, 2048, 512, 512, 512


def setup_inputs():
    n = np.random.standard_normal
    s = mx_kscale(K)[:, None]
    u = mx_kscale(H)
    packed_xT = pack_weight(n((K, T)) * s)
    packed_w1 = pack_fp4(n((K, H)) / np.sqrt(2 * K) / s)
    packed_w2 = pack_fp4(n((K, H)) / np.sqrt(2 * K) / s)
    packed_w3 = pack_fp4(n((H, N)) / np.sqrt(H) / u[:, None])
    return {
        "x_words": packed_xT[0],
        "x_scales": packed_xT[1],
        "w1_words": packed_w1[0],
        "w1_scales": packed_w1[1],
        "w2_words": packed_w2[0],
        "w2_scales": packed_w2[1],
        "gn": (np.random.uniform(0.5, 1.5, (H, 1)) * u[:, None]).astype(np.float32),
        "w3_words": packed_w3[0],
        "w3_scales": packed_w3[1],
        "offs": striped(np.random.permutation(T)[:S]),
        "c1": striped(np.random.permutation(T)[:S]),
        "c2": striped(np.random.permutation(T)[:S]),
        "mate": striped8(np.stack([np.random.permutation(S) for _ in range(8)])),
    }


def reference(x_words, x_scales, w1_words, w1_scales, w2_words, w2_scales, gn, w3_words, w3_scales, offs, c1, c2, mate):
    xq = unpack_weight(x_words, x_scales)[:, unstriped(offs)]
    x_c1 = unpack_weight(x_words, x_scales)[:, unstriped(c1)]
    w1q = unpack_fp4(w1_words, w1_scales)
    w2q = unpack_fp4(w2_words, w2_scales)
    y = w1q.T @ xq + w2q.T @ x_c1
    x_c2 = unpack_weight(x_words, x_scales)[:, unstriped(c2)]
    e = w1q.T @ x_c1 + w2q.T @ x_c2
    mx = relu(np.maximum(y, e))
    z = f64(gn) * (mx + mx[np.arange(H)[:, None], runs(mate, H)])
    out_0 = unpack_fp4(w3_words, w3_scales).T @ mxq(z, 0, "e4m3")
    return (out_0,) + planes(out_0)

@@ -1,0 +1,241 @@
+from contextlib import ExitStack
+
+import concourse.mybir as mybir
+from concourse.masks import make_identity
+
+K, T, S, H, N = 512, 2048, 512, 512, 512
+FLOPS = 2 * (4 * K * H * S + H * N * S)
+
+F32 = mybir.dt.float32
+BF16 = mybir.dt.bfloat16
+I32 = mybir.dt.int32
+U32 = mybir.dt.uint32
+U16 = mybir.dt.uint16
+U8 = mybir.dt.uint8
+FP8X4 = mybir.dt.float8_e4m3fn_x4
+FP4X4 = mybir.dt.float4_e2m1fn_x4
+ALU = mybir.AluOpType
+ACT = mybir.ActivationFunctionType
+
+P = 128
+PACK = 4
+QUADS = 4
+HALF = S // 2
+CHUNK = 128
+LIST_COLS = S // 16
+
+
+def load_scale_rows(queues, plane, rows):
+    for q in range(QUADS):
+        queues[q % len(queues)].dma_start(out=plane[32 * q : 32 * q + 4, :].bitcast(I32), in_=rows[0, 4 * q : 4 * q + 4, :].bitcast(I32))
+
+
+def interleaved(dst, src):
+    return (
+        dst.rearrange("p (c i t) -> p c t i", i=4, t=PACK),
+        src.rearrange("p t (c i) -> p c t i", i=4),
+    )
+
+
+def tile_picked_charcnn_relu_po_kernel(
+    tc, x_words, x_scales, w1_words, w1_scales, w2_words, w2_scales, gn, w3_words, w3_scales,
+    offs, c1, c2, mate, out_0, out_1, out_2,
+):
+    nc = tc.nc
+    with ExitStack() as ctx:
+        held = ctx.enter_context(tc.tile_pool(name="held", bufs=1))
+        psum = ctx.enter_context(tc.psum_pool(name="psum", bufs=1))
+
+        def sb(name, shape, dtype, tag=None):
+            return held.tile(shape, dtype, name=name, tag=tag or name, align_bytes=64)
+
+        def bank(index, shape):
+            return psum.tile(shape, F32, name="bank%d" % index)
+
+        lists = {}
+        for name in ("c1", "offs", "c2", "mate"):
+            lists[name] = held.tile([P, LIST_COLS], U16, name="list_" + name)
+
+        x_plane = sb("x_plane", [P, T], U8)
+        x_table = sb("x_table", [P, T], I32)
+        w_plane = [sb("w_plane%d" % i, [P, H], U8) for i in range(3)]
+        w_codes = [sb("w_codes%d" % i, [P, 2 * H], U8) for i in range(3)]
+        gain = sb("gain", [P, PACK], F32)
+        ident = sb("ident", [P, P], F32)
+        warm = sb("warm", [P, 1], F32)
+
+        nc.gpsimd.memset(x_plane[:].bitcast(I32), 0)
+        nc.vector.memset(w_plane[1][:].bitcast(I32), 0)
+        nc.vector.memset(w_plane[0][:].bitcast(I32), 0)
+        nc.vector.memset(w_plane[2][:].bitcast(I32), 0)
+
+        nc.sync.dma_start(lists["c1"][:], c1)
+        load_scale_rows([nc.sync, nc.scalar], x_plane, x_scales)
+        nc.sync.dma_start(lists["offs"][:], offs)
+        nc.sync.dma_start(out=x_table[:], in_=x_words[0].rearrange("p n t -> p (n t)").bitcast(I32))
+        nc.sync.dma_start(out=w_codes[1][:].bitcast(I32), in_=w2_words[0].bitcast(I32))
+        load_scale_rows([nc.sync], w_plane[1], w2_scales)
+        nc.sync.dma_start(lists["c2"][:], c2)
+        nc.sync.dma_start(out=w_codes[0][:].bitcast(I32), in_=w1_words[0].bitcast(I32))
+        nc.sync.dma_start(lists["mate"][:], mate)
+        load_scale_rows([nc.sync], w_plane[0], w1_scales)
+        nc.sync.dma_start(out=gain[:], in_=gn.rearrange("(p t) o -> p (t o)", t=PACK))
+        nc.sync.dma_start(out=w_codes[2][:].bitcast(I32), in_=w3_words[0].bitcast(I32))
+        load_scale_rows([nc.sync], w_plane[2], w3_scales)
+
+        make_identity(nc, ident[:])
+        nc.scalar.activation(out=warm[:], in_=ident[:, 0:1], func=ACT.Relu)
+
+        picked_scales = {}
+        picked_words = {}
+
+        def gather_scales(name):
+            picked_scales[name] = sb("scales_" + name, [P, S], U8)
+            nc.vector.tensor_copy(picked_scales[name][:], x_plane[:].indirect(lists[name][:]))
+
+        def gather_words(name, h):
+            picked_words[name, h] = sb("words_%s%d" % (name, h), [P, HALF], U32)
+            cols = slice(h * LIST_COLS // 2, (h + 1) * LIST_COLS // 2)
+            nc.vector.tensor_copy(picked_words[name, h][:], x_table[:].bitcast(U32).indirect(lists[name][:, cols]))
+
+        def first_layer_pass(acc, name, b, w, start):
+            h, r = divmod(b, 2)
+            nc.tensor.matmul_mx(
+                out=acc[:],
+                lhsT=picked_words[name, h][:, r * P : (r + 1) * P].bitcast(FP8X4),
+                lhsT_scale=picked_scales[name][:, b * P : (b + 1) * P],
+                rhs=w_codes[w][:].bitcast(FP4X4),
+                rhs_scale=w_plane[w][:],
+                start=start,
+                stop=not start,
+            )
+
+        gather_scales("c1")
+        gather_scales("offs")
+        gather_words("c1", 0)
+        gather_words("c1", 1)
+        gather_words("offs", 0)
+        gather_words("offs", 1)
+        gather_scales("c2")
+        gather_words("c2", 0)
+        gather_words("c2", 1)
+
+        y_acc = [bank(b, [P, H]) for b in range(4)]
+        e_acc = [bank(4 + b, [P, H]) for b in range(4)]
+        for b in range(4):
+            first_layer_pass(y_acc[b], "c1", b, 1, True)
+        relu_y = []
+        for b in range(4):
+            first_layer_pass(y_acc[b], "offs", b, 0, False)
+            relu_y.append(sb("relu_y%d" % b, [P, PACK, P], F32))
+            nc.scalar.activation(out=relu_y[b][:], in_=y_acc[b][:].rearrange("p (m t) -> p t m", t=PACK), func=ACT.Relu)
+
+        largest = []
+        for b in range(4):
+            first_layer_pass(e_acc[b], "c1", b, 0, True)
+            first_layer_pass(e_acc[b], "c2", b, 1, False)
+            largest.append(sb("largest%d" % b, [P, PACK, P], F32))
+            nc.vector.tensor_tensor(
+                out=largest[b][:], in0=e_acc[b][:].rearrange("p (m t) -> p t m", t=PACK), in1=relu_y[b][:], op=ALU.max
+            )
+
+        turned = [bank(t, [P, S]) for t in range(PACK)]
+        for b in range(4):
+            for t in range(PACK):
+                nc.tensor.transpose(turned[t][:, b * P : (b + 1) * P], largest[b][:, t, :], ident[:])
+
+        w3_codes = sb("w3_codes", [P, 2 * N], U8, tag="relu_y3")
+        w3_plane = sb("w3_plane", [P, N], U8, tag="relu_y2")
+        nc.vector.tensor_copy(
+            out=w3_codes[:].rearrange("p (t m b) -> p t m b", t=PACK, b=2),
+            in_=w_codes[2][:].rearrange("p (m t b) -> p t m b", t=PACK, b=2),
+        )
+        nc.vector.tensor_copy(
+            out=w3_plane[:].rearrange("p (t m) -> p t m", t=PACK),
+            in_=w_plane[2][:].rearrange("p (m t) -> p t m", t=PACK),
+        )
+
+        sums = [sb("sums%d" % h, [P, PACK, HALF], F32) for h in range(2)]
+        window = [sb("window%d" % t, [P, S], F32) for t in range(PACK)]
+        own = {t: [sb("own%d_%d" % (t, h), [P, HALF], F32) for h in range(2)] for t in range(2, PACK)}
+        both = [sb("both%d" % t, [P, S], F32) for t in range(2)]
+
+        def scaled(dst, t, cols):
+            nc.scalar.activation(out=dst, in_=turned[t][:, cols], func=ACT.Copy, scale=gain[:, t : t + 1])
+
+        def add_mates(t, h, plain):
+            cols = slice(h * LIST_COLS // 2, (h + 1) * LIST_COLS // 2)
+            nc.vector.tensor_tensor(
+                out=sums[h][:, t, :], in0=window[t][:].indirect(lists["mate"][:, cols]), in1=plain, op=ALU.add
+            )
+
+        halves = [slice(0, HALF), slice(HALF, S)]
+        for t in range(2):
+            scaled(window[t][:], t, slice(0, S))
+            nc.vector.tensor_copy(out=both[t][:], in_=window[t][:])
+            for h in range(2):
+                add_mates(t, h, both[t][:, halves[h]])
+        for t in range(2, PACK):
+            scaled(window[t][:], t, slice(0, S))
+            scaled(own[t][0][:], t, halves[0])
+            add_mates(t, 0, own[t][0][:])
+        for t in range(2, PACK):
+            scaled(own[t][1][:], t, halves[1])
+            add_mates(t, 1, own[t][1][:])
+
+        z_words = {}
+        z_scales = {}
+        z_bf = {}
+
+        def round_z(copy, c, tag=None):
+            h, r = divmod(c, 2)
+            z_bf[c] = sb("z_bf%d" % c, [P, PACK * CHUNK], BF16, tag=tag)
+            dst, src = interleaved(z_bf[c][:], sums[h][:, :, r * CHUNK : (r + 1) * CHUNK])
+            copy(out=dst, in_=src)
+
+        def quantise_z(c):
+            z_words[c] = sb("z_words%d" % c, [P, CHUNK], U32)
+            z_scales[c] = sb("z_scales%d" % c, [P, CHUNK], U8)
+            nc.vector.quantize_mx(out=z_words[c][:].bitcast(FP8X4), scales=z_scales[c][:], in_=z_bf[c][:])
+
+        round_z(nc.scalar.copy, 0)
+        round_z(nc.scalar.copy, 1)
+        round_z(nc.scalar.copy, 3)
+        quantise_z(0)
+        round_z(nc.vector.tensor_copy, 2, tag="z_bf0")
+        quantise_z(1)
+        quantise_z(2)
+        quantise_z(3)
+
+        out_rows = out_0.rearrange("(p t) j -> p t j", t=PACK)
+        out_words = out_1[0].rearrange("p n t -> p (n t)").bitcast(I32)
+        y_scales = sb("y_scales", [P, S], U8)
+        y_words = [sb("y_words%d" % h, [P, HALF], U32) for h in range(2)]
+        for c in range(S // CHUNK):
+            acc = bank(4 + c, [P, PACK, CHUNK])
+            for t in range(PACK):
+                nc.tensor.matmul_mx(
+                    out=acc[:, t, :],
+                    lhsT=w3_codes[:, 2 * t * P : 2 * (t + 1) * P].bitcast(FP4X4),
+                    lhsT_scale=w3_plane[:, t * P : (t + 1) * P],
+                    rhs=z_words[c][:].bitcast(FP8X4),
+                    rhs_scale=z_scales[c][:],
+                    start=True,
+                    stop=True,
+                )
+            cols = slice(c * CHUNK, (c + 1) * CHUNK)
+            result = sb("result%d" % c, [P, PACK, CHUNK], F32)
+            nc.scalar.copy(out=result[:], in_=acc[:])
+            nc.sync.dma_start(out=out_rows[:, :, cols], in_=result[:])
+            result_bf = sb("result_bf%d" % c, [P, PACK * CHUNK], BF16)
+            dst, src = interleaved(result_bf[:], result[:])
+            nc.vector.tensor_copy(out=dst, in_=src)
+            h, r = divmod(c, 2)
+            nc.vector.quantize_mx(
+                out=y_words[h][:, r * CHUNK : (r + 1) * CHUNK].bitcast(FP8X4), scales=y_scales[:, cols], in_=result_bf[:]
+            )
+            if r == 1:
+                nc.sync.dma_start(out=out_words[:, h * HALF : (h + 1) * HALF], in_=y_words[h][:].bitcast(I32))
+        for q in range(QUADS):
+            queue = nc.scalar if q % 2 else nc.sync
+            queue.dma_start(out=out_2[0, 4 * q : 4 * q + 4, :].bitcast(I32), in_=y_scales[32 * q : 32 * q + 4, :].bitcast(I32))

@@ -93,16 +93,18 @@ def tile_picked_charcnn_relu_po_kernel(
             picked_scales[name] = sb("scales_" + name, [P, S], U8)
             nc.vector.tensor_copy(picked_scales[name][:], x_plane[:].indirect(lists[name][:]))
 
-        def gather_words(name, h):
-            picked_words[name, h] = sb("words_%s%d" % (name, h), [P, HALF], U32)
-            cols = slice(h * LIST_COLS // 2, (h + 1) * LIST_COLS // 2)
-            nc.vector.tensor_copy(picked_words[name, h][:], x_table[:].bitcast(U32).indirect(lists[name][:, cols]))
+        def gather_words(name, pieces):
+            picked_words[name] = []
+            for i in range(pieces):
+                picked = sb("words_%s%d" % (name, i), [P, S // pieces], U32)
+                cols = slice(i * LIST_COLS // pieces, (i + 1) * LIST_COLS // pieces)
+                nc.vector.tensor_copy(picked[:], x_table[:].bitcast(U32).indirect(lists[name][:, cols]))
+                picked_words[name].extend(picked[:, r * P : (r + 1) * P] for r in range(4 // pieces))
 
         def first_layer_pass(acc, name, b, w, start):
-            h, r = divmod(b, 2)
             nc.tensor.matmul_mx(
                 out=acc[:],
-                lhsT=picked_words[name, h][:, r * P : (r + 1) * P].bitcast(FP8X4),
+                lhsT=picked_words[name][b].bitcast(FP8X4),
                 lhsT_scale=picked_scales[name][:, b * P : (b + 1) * P],
                 rhs=w_codes[w][:].bitcast(FP4X4),
                 rhs_scale=w_plane[w][:],
@@ -112,23 +114,21 @@ def tile_picked_charcnn_relu_po_kernel(
 
         gather_scales("c1")
         gather_scales("offs")
-        gather_words("c1", 0)
-        gather_words("c1", 1)
-        gather_words("offs", 0)
+        gather_words("c1", 2)
         gather_words("offs", 1)
         gather_scales("c2")
-        gather_words("c2", 0)
-        gather_words("c2", 1)
+        gather_words("c2", 2)
 
         y_acc = [bank(b, [P, H]) for b in range(4)]
         e_acc = [bank(4 + b, [P, H]) for b in range(4)]
         for b in range(4):
             first_layer_pass(y_acc[b], "c1", b, 1, True)
-        relu_y = []
+        window = [sb("window%d" % t, [P, 2 * S if t < 2 else S], F32) for t in range(PACK)]
+        relu_y = [window[b][:, S:] if b < 2 else sb("relu_y%d" % b, [P, H], F32)[:] for b in range(4)]
+        relu_y = [rows.rearrange("p (t m) -> p t m", t=PACK) for rows in relu_y]
         for b in range(4):
             first_layer_pass(y_acc[b], "offs", b, 0, False)
-            relu_y.append(sb("relu_y%d" % b, [P, PACK, P], F32))
-            nc.scalar.activation(out=relu_y[b][:], in_=y_acc[b][:].rearrange("p (m t) -> p t m", t=PACK), func=ACT.Relu)
+            nc.scalar.activation(out=relu_y[b], in_=y_acc[b][:].rearrange("p (m t) -> p t m", t=PACK), func=ACT.Relu)
 
         largest = []
         for b in range(4):
@@ -136,13 +136,15 @@ def tile_picked_charcnn_relu_po_kernel(
             first_layer_pass(e_acc[b], "c2", b, 1, False)
             largest.append(sb("largest%d" % b, [P, PACK, P], F32))
             nc.vector.tensor_tensor(
-                out=largest[b][:], in0=e_acc[b][:].rearrange("p (m t) -> p t m", t=PACK), in1=relu_y[b][:], op=ALU.max
+                out=largest[b][:], in0=e_acc[b][:].rearrange("p (m t) -> p t m", t=PACK), in1=relu_y[b], op=ALU.max
             )
 
         turned = [bank(t, [P, S]) for t in range(PACK)]
+        turned_late = {b: bank(2 + b, [P, P]) for b in (2, 3)}
         for b in range(4):
             for t in range(PACK):
-                nc.tensor.transpose(turned[t][:, b * P : (b + 1) * P], largest[b][:, t, :], ident[:])
+                dst = turned_late[b][:] if t == 0 and b in turned_late else turned[t][:, b * P : (b + 1) * P]
+                nc.tensor.transpose(dst, largest[b][:, t, :], ident[:])
 
         w3_codes = sb("w3_codes", [P, 2 * N], U8, tag="relu_y3")
         w3_plane = sb("w3_plane", [P, N], U8, tag="relu_y2")
@@ -155,42 +157,46 @@ def tile_picked_charcnn_relu_po_kernel(
             in_=w_plane[2][:].rearrange("p (m t) -> p t m", t=PACK),
         )
 
-        sums = [sb("sums%d" % h, [P, PACK, HALF], F32) for h in range(2)]
-        window = [sb("window%d" % t, [P, S], F32) for t in range(PACK)]
+        sums = sb("sums", [P, PACK, S], F32)
         own = {t: [sb("own%d_%d" % (t, h), [P, HALF], F32) for h in range(2)] for t in range(2, PACK)}
-        both = [sb("both%d" % t, [P, S], F32) for t in range(2)]
+        own_all = [sb("own_all%d" % t, [P, S], F32) for t in range(2)]
+
+        def scaled_from(dst, t, src):
+            nc.scalar.activation(out=dst, in_=src, func=ACT.Copy, scale=gain[:, t : t + 1])
 
         def scaled(dst, t, cols):
-            nc.scalar.activation(out=dst, in_=turned[t][:, cols], func=ACT.Copy, scale=gain[:, t : t + 1])
+            scaled_from(dst, t, turned[t][:, cols])
 
-        def add_mates(t, h, plain):
-            cols = slice(h * LIST_COLS // 2, (h + 1) * LIST_COLS // 2)
-            nc.vector.tensor_tensor(
-                out=sums[h][:, t, :], in0=window[t][:].indirect(lists["mate"][:, cols]), in1=plain, op=ALU.add
-            )
+        def add_mates(t, cols, plain):
+            entries = lists["mate"][:, cols.start // 16 : cols.stop // 16]
+            nc.vector.tensor_tensor(out=sums[:, t, cols], in0=window[t][:].indirect(entries), in1=plain, op=ALU.add)
 
         halves = [slice(0, HALF), slice(HALF, S)]
-        for t in range(2):
-            scaled(window[t][:], t, slice(0, S))
-            nc.vector.tensor_copy(out=both[t][:], in_=window[t][:])
-            for h in range(2):
-                add_mates(t, h, both[t][:, halves[h]])
+        whole = slice(0, S)
+        scaled(window[0][:, halves[0]], 0, halves[0])
+        scaled(own_all[0][:, halves[0]], 0, halves[0])
+        for b in turned_late:
+            scaled_from(window[0][:, b * P : (b + 1) * P], 0, turned_late[b][:])
+            scaled_from(own_all[0][:, b * P : (b + 1) * P], 0, turned_late[b][:])
+        add_mates(0, whole, own_all[0][:])
+        scaled(window[1][:, whole], 1, whole)
+        scaled(own_all[1][:], 1, whole)
+        add_mates(1, whole, own_all[1][:])
         for t in range(2, PACK):
             scaled(window[t][:], t, slice(0, S))
             scaled(own[t][0][:], t, halves[0])
-            add_mates(t, 0, own[t][0][:])
+            add_mates(t, halves[0], own[t][0][:])
         for t in range(2, PACK):
             scaled(own[t][1][:], t, halves[1])
-            add_mates(t, 1, own[t][1][:])
+            add_mates(t, halves[1], own[t][1][:])
 
         z_words = {}
         z_scales = {}
         z_bf = {}
 
         def round_z(copy, c, tag=None):
-            h, r = divmod(c, 2)
             z_bf[c] = sb("z_bf%d" % c, [P, PACK * CHUNK], BF16, tag=tag)
-            dst, src = interleaved(z_bf[c][:], sums[h][:, :, r * CHUNK : (r + 1) * CHUNK])
+            dst, src = interleaved(z_bf[c][:], sums[:, :, c * CHUNK : (c + 1) * CHUNK])
             copy(out=dst, in_=src)
 
         def quantise_z(c):
@@ -210,7 +216,8 @@ def tile_picked_charcnn_relu_po_kernel(
         out_rows = out_0.rearrange("(p t) j -> p t j", t=PACK)
         out_words = out_1[0].rearrange("p n t -> p (n t)").bitcast(I32)
         y_scales = sb("y_scales", [P, S], U8)
-        y_words = [sb("y_words%d" % h, [P, HALF], U32) for h in range(2)]
+        y_words = sb("y_words", [P, S], U32)
+        result_bf = [sb("result_bf%d" % h, [P, PACK * HALF], BF16) for h in range(2)]
         for c in range(S // CHUNK):
             acc = bank(4 + c, [P, PACK, CHUNK])
             for t in range(PACK):
@@ -227,15 +234,14 @@ def tile_picked_charcnn_relu_po_kernel(
             result = sb("result%d" % c, [P, PACK, CHUNK], F32)
             nc.scalar.copy(out=result[:], in_=acc[:])
             nc.sync.dma_start(out=out_rows[:, :, cols], in_=result[:])
-            result_bf = sb("result_bf%d" % c, [P, PACK * CHUNK], BF16)
-            dst, src = interleaved(result_bf[:], result[:])
-            nc.vector.tensor_copy(out=dst, in_=src)
             h, r = divmod(c, 2)
-            nc.vector.quantize_mx(
-                out=y_words[h][:, r * CHUNK : (r + 1) * CHUNK].bitcast(FP8X4), scales=y_scales[:, cols], in_=result_bf[:]
-            )
+            dst, src = interleaved(result_bf[h][:, r * PACK * CHUNK : (r + 1) * PACK * CHUNK], result[:])
+            nc.vector.tensor_copy(out=dst, in_=src)
             if r == 1:
-                nc.sync.dma_start(out=out_words[:, h * HALF : (h + 1) * HALF], in_=y_words[h][:].bitcast(I32))
+                nc.vector.quantize_mx(
+                    out=y_words[:, halves[h]].bitcast(FP8X4), scales=y_scales[:, halves[h]], in_=result_bf[h][:]
+                )
+        nc.sync.dma_start(out=out_words, in_=y_words[:].bitcast(I32))
         for q in range(QUADS):
             queue = nc.scalar if q % 2 else nc.sync
             queue.dma_start(out=out_2[0, 4 * q : 4 * q + 4, :].bitcast(I32), in_=y_scales[32 * q : 32 * q + 4, :].bitcast(I32))

@@ -134,25 +134,32 @@ def tile_picked_charcnn_relu_po_kernel(
         for b in range(4):
             first_layer_pass(e_acc[b], "c1", b, 0, True)
             first_layer_pass(e_acc[b], "c2", b, 1, False)
-            largest.append(sb("largest%d" % b, [P, PACK, P], F32))
-            nc.vector.tensor_tensor(
-                out=largest[b][:], in0=e_acc[b][:].rearrange("p (m t) -> p t m", t=PACK), in1=relu_y[b], op=ALU.max
-            )
+            rows = []
+            for part in ([slice(0, PACK)] if b < 3 else [slice(0, 1), slice(1, PACK)]):
+                piece = sb("largest%d_%d" % (b, part.start), [P, part.stop - part.start, P], F32)
+                nc.vector.tensor_tensor(
+                    out=piece[:],
+                    in0=e_acc[b][:].rearrange("p (m t) -> p t m", t=PACK)[:, part, :],
+                    in1=relu_y[b][:, part, :],
+                    op=ALU.max,
+                )
+                rows.extend(piece[:, i, :] for i in range(part.stop - part.start))
+            largest.append(rows)
 
         turned = [bank(t, [P, S]) for t in range(PACK)]
         turned_late = {b: bank(2 + b, [P, P]) for b in (2, 3)}
-        for b in range(4):
-            for t in range(PACK):
+        for t in range(PACK):
+            for b in range(4):
                 dst = turned_late[b][:] if t == 0 and b in turned_late else turned[t][:, b * P : (b + 1) * P]
-                nc.tensor.transpose(dst, largest[b][:, t, :], ident[:])
+                nc.tensor.transpose(dst, largest[b][t], ident[:])
 
-        w3_codes = sb("w3_codes", [P, 2 * N], U8, tag="relu_y3")
-        w3_plane = sb("w3_plane", [P, N], U8, tag="relu_y2")
-        nc.vector.tensor_copy(
+        w3_codes = sb("w3_codes", [P, 2 * N], U8, tag="x_table")
+        w3_plane = sb("w3_plane", [P, N], U8, tag="words_c11")
+        nc.gpsimd.tensor_copy(
             out=w3_codes[:].rearrange("p (t m b) -> p t m b", t=PACK, b=2),
             in_=w_codes[2][:].rearrange("p (m t b) -> p t m b", t=PACK, b=2),
         )
-        nc.vector.tensor_copy(
+        nc.gpsimd.tensor_copy(
             out=w3_plane[:].rearrange("p (t m) -> p t m", t=PACK),
             in_=w_plane[2][:].rearrange("p (m t) -> p t m", t=PACK),
         )

@@ -153,8 +153,8 @@ def tile_picked_charcnn_relu_po_kernel(
                 dst = turned_late[b][:] if t == 0 and b in turned_late else turned[t][:, b * P : (b + 1) * P]
                 nc.tensor.transpose(dst, largest[b][t], ident[:])
 
-        w3_codes = sb("w3_codes", [P, 2 * N], U8, tag="x_table")
-        w3_plane = sb("w3_plane", [P, N], U8, tag="words_c11")
+        w3_codes = sb("w3_codes", [P, 2 * N], U8)
+        w3_plane = sb("w3_plane", [P, N], U8)
         nc.gpsimd.tensor_copy(
             out=w3_codes[:].rearrange("p (t m b) -> p t m b", t=PACK, b=2),
             in_=w_codes[2][:].rearrange("p (m t b) -> p t m b", t=PACK, b=2),

@@ -1,7 +1,6 @@
 from contextlib import ExitStack
 
 import concourse.mybir as mybir
-from concourse.masks import make_identity
 
 K, T, S, H, N = 512, 2048, 512, 512, 512
 FLOPS = 2 * (4 * K * H * S + H * N * S)
@@ -23,11 +22,6 @@ QUADS = 4
 HALF = S // 2
 CHUNK = 128
 LIST_COLS = S // 16
-
-
-def load_scale_rows(queues, plane, rows):
-    for q in range(QUADS):
-        queues[q % len(queues)].dma_start(out=plane[32 * q : 32 * q + 4, :].bitcast(I32), in_=rows[0, 4 * q : 4 * q + 4, :].bitcast(I32))
 
 
 def interleaved(dst, src):
@@ -58,33 +52,59 @@ def tile_picked_charcnn_relu_po_kernel(
 
         x_plane = sb("x_plane", [P, T], U8)
         x_table = sb("x_table", [P, T], I32)
-        w_plane = [sb("w_plane%d" % i, [P, H], U8) for i in range(3)]
-        w_codes = [sb("w_codes%d" % i, [P, 2 * H], U8) for i in range(3)]
+        raw_plane = {w: sb("raw_plane%d" % w, [P, H], U8) for w in (1, 2, 3)}
+        raw_codes = {w: sb("raw_codes%d" % w, [P, 2 * H], U8) for w in (1, 2, 3)}
         gain = sb("gain", [P, PACK], F32)
-        ident = sb("ident", [P, P], F32)
-        warm = sb("warm", [P, 1], F32)
 
-        nc.gpsimd.memset(x_plane[:].bitcast(I32), 0)
-        nc.vector.memset(w_plane[1][:].bitcast(I32), 0)
-        nc.vector.memset(w_plane[0][:].bitcast(I32), 0)
-        nc.vector.memset(w_plane[2][:].bitcast(I32), 0)
+        nc.vector.memset(x_plane[:, : T // 2].bitcast(I32), 0)
+        nc.gpsimd.memset(x_plane[:, T // 2 :].bitcast(I32), 0)
+        for w in (2, 1, 3):
+            nc.vector.memset(raw_plane[w][:].bitcast(I32), 0)
+
+        def load_scale_rows(plane, rows, quads):
+            for q in quads:
+                nc.sync.dma_start(
+                    out=plane[32 * q : 32 * q + 4, :].bitcast(I32), in_=rows[0, 4 * q : 4 * q + 4, :].bitcast(I32)
+                )
+
+        def load_codes(w, words):
+            nc.sync.dma_start(out=raw_codes[w][:].bitcast(I32), in_=words[0].bitcast(I32))
 
         nc.sync.dma_start(lists["c1"][:], c1)
-        load_scale_rows([nc.sync, nc.scalar], x_plane, x_scales)
         nc.sync.dma_start(lists["offs"][:], offs)
+        load_codes(2, w2_words)
+        load_scale_rows(x_plane, x_scales, range(QUADS))
         nc.sync.dma_start(out=x_table[:], in_=x_words[0].rearrange("p n t -> p (n t)").bitcast(I32))
-        nc.sync.dma_start(out=w_codes[1][:].bitcast(I32), in_=w2_words[0].bitcast(I32))
-        load_scale_rows([nc.sync], w_plane[1], w2_scales)
+        load_scale_rows(raw_plane[2], w2_scales, range(QUADS))
+        load_codes(1, w1_words)
+        load_scale_rows(raw_plane[1], w1_scales, (0, 1))
         nc.sync.dma_start(lists["c2"][:], c2)
-        nc.sync.dma_start(out=w_codes[0][:].bitcast(I32), in_=w1_words[0].bitcast(I32))
-        nc.sync.dma_start(lists["mate"][:], mate)
-        load_scale_rows([nc.sync], w_plane[0], w1_scales)
+        load_scale_rows(raw_plane[1], w1_scales, (2, 3))
         nc.sync.dma_start(out=gain[:], in_=gn.rearrange("(p t) o -> p (t o)", t=PACK))
-        nc.sync.dma_start(out=w_codes[2][:].bitcast(I32), in_=w3_words[0].bitcast(I32))
-        load_scale_rows([nc.sync], w_plane[2], w3_scales)
+        nc.sync.dma_start(lists["mate"][:], mate)
+        load_codes(3, w3_words)
+        load_scale_rows(raw_plane[3], w3_scales, range(QUADS))
 
-        make_identity(nc, ident[:])
-        nc.scalar.activation(out=warm[:], in_=ident[:, 0:1], func=ACT.Relu)
+        codes = {}
+        plane = {}
+
+        def deal_codes(w):
+            codes[w] = sb("codes%d" % w, [P, 2 * H], U8)
+            nc.gpsimd.tensor_copy(
+                out=codes[w][:].rearrange("p (t m b) -> p t m b", t=PACK, b=2),
+                in_=raw_codes[w][:].rearrange("p (m t b) -> p t m b", t=PACK, b=2),
+            )
+
+        def deal_plane(w):
+            plane[w] = sb("plane%d" % w, [P, H], U8)
+            nc.gpsimd.tensor_copy(
+                out=plane[w][:].rearrange("p (t m) -> p t m", t=PACK),
+                in_=raw_plane[w][:].rearrange("p (m t) -> p t m", t=PACK),
+            )
+
+        for w in (2, 1, 3):
+            deal_codes(w)
+            deal_plane(w)
 
         picked_scales = {}
         picked_words = {}
@@ -93,117 +113,74 @@ def tile_picked_charcnn_relu_po_kernel(
             picked_scales[name] = sb("scales_" + name, [P, S], U8)
             nc.vector.tensor_copy(picked_scales[name][:], x_plane[:].indirect(lists[name][:]))
 
-        def gather_words(name, pieces):
-            picked_words[name] = []
-            for i in range(pieces):
-                picked = sb("words_%s%d" % (name, i), [P, S // pieces], U32)
-                cols = slice(i * LIST_COLS // pieces, (i + 1) * LIST_COLS // pieces)
-                nc.vector.tensor_copy(picked[:], x_table[:].bitcast(U32).indirect(lists[name][:, cols]))
-                picked_words[name].extend(picked[:, r * P : (r + 1) * P] for r in range(4 // pieces))
+        def gather_words(name):
+            picked_words[name] = sb("words_" + name, [P, S], U32)
+            nc.vector.tensor_copy(picked_words[name][:], x_table[:].bitcast(U32).indirect(lists[name][:]))
 
-        def first_layer_pass(acc, name, b, w, start):
+        def mx_pass(acc, w, t, words, scales, start, stop):
             nc.tensor.matmul_mx(
-                out=acc[:],
-                lhsT=picked_words[name][b].bitcast(FP8X4),
-                lhsT_scale=picked_scales[name][:, b * P : (b + 1) * P],
-                rhs=w_codes[w][:].bitcast(FP4X4),
-                rhs_scale=w_plane[w][:],
+                out=acc,
+                lhsT=codes[w][:, 2 * t * P : 2 * (t + 1) * P].bitcast(FP4X4),
+                lhsT_scale=plane[w][:, t * P : (t + 1) * P],
+                rhs=words.bitcast(FP8X4),
+                rhs_scale=scales,
                 start=start,
-                stop=not start,
+                stop=stop,
             )
+
+        def first_layer_pass(acc, w, t, name, start):
+            mx_pass(acc[:], w, t, picked_words[name][:], picked_scales[name][:], start, not start)
 
         gather_scales("c1")
         gather_scales("offs")
-        gather_words("c1", 2)
-        gather_words("offs", 1)
+        gather_words("c1")
+        gather_words("offs")
         gather_scales("c2")
-        gather_words("c2", 2)
+        gather_words("c2")
 
-        y_acc = [bank(b, [P, H]) for b in range(4)]
-        e_acc = [bank(4 + b, [P, H]) for b in range(4)]
-        for b in range(4):
-            first_layer_pass(y_acc[b], "c1", b, 1, True)
-        window = [sb("window%d" % t, [P, 2 * S if t < 2 else S], F32) for t in range(PACK)]
-        relu_y = [window[b][:, S:] if b < 2 else sb("relu_y%d" % b, [P, H], F32)[:] for b in range(4)]
-        relu_y = [rows.rearrange("p (t m) -> p t m", t=PACK) for rows in relu_y]
-        for b in range(4):
-            first_layer_pass(y_acc[b], "offs", b, 0, False)
-            nc.scalar.activation(out=relu_y[b], in_=y_acc[b][:].rearrange("p (m t) -> p t m", t=PACK), func=ACT.Relu)
-
-        largest = []
-        for b in range(4):
-            first_layer_pass(e_acc[b], "c1", b, 0, True)
-            first_layer_pass(e_acc[b], "c2", b, 1, False)
-            rows = []
-            for part in ([slice(0, PACK)] if b < 3 else [slice(0, 1), slice(1, PACK)]):
-                piece = sb("largest%d_%d" % (b, part.start), [P, part.stop - part.start, P], F32)
-                nc.vector.tensor_tensor(
-                    out=piece[:],
-                    in0=e_acc[b][:].rearrange("p (m t) -> p t m", t=PACK)[:, part, :],
-                    in1=relu_y[b][:, part, :],
-                    op=ALU.max,
-                )
-                rows.extend(piece[:, i, :] for i in range(part.stop - part.start))
-            largest.append(rows)
-
-        turned = [bank(t, [P, S]) for t in range(PACK)]
-        turned_late = {b: bank(2 + b, [P, P]) for b in (2, 3)}
+        y_acc = [bank(t, [P, S]) for t in range(PACK)]
+        e_acc = [bank(4 + t, [P, S]) for t in range(PACK)]
         for t in range(PACK):
-            for b in range(4):
-                dst = turned_late[b][:] if t == 0 and b in turned_late else turned[t][:, b * P : (b + 1) * P]
-                nc.tensor.transpose(dst, largest[b][t], ident[:])
+            first_layer_pass(y_acc[t], 2, t, "c1", True)
+        relu_y = [sb("relu_y%d" % t, [P, S], F32) for t in range(PACK)]
+        for t in range(PACK):
+            first_layer_pass(y_acc[t], 1, t, "offs", False)
+            nc.scalar.activation(out=relu_y[t][:], in_=y_acc[t][:], func=ACT.Relu)
 
-        w3_codes = sb("w3_codes", [P, 2 * N], U8)
-        w3_plane = sb("w3_plane", [P, N], U8)
-        nc.gpsimd.tensor_copy(
-            out=w3_codes[:].rearrange("p (t m b) -> p t m b", t=PACK, b=2),
-            in_=w_codes[2][:].rearrange("p (m t b) -> p t m b", t=PACK, b=2),
-        )
-        nc.gpsimd.tensor_copy(
-            out=w3_plane[:].rearrange("p (t m) -> p t m", t=PACK),
-            in_=w_plane[2][:].rearrange("p (m t) -> p t m", t=PACK),
-        )
-
-        sums = sb("sums", [P, PACK, S], F32)
-        own = {t: [sb("own%d_%d" % (t, h), [P, HALF], F32) for h in range(2)] for t in range(2, PACK)}
-        own_all = [sb("own_all%d" % t, [P, S], F32) for t in range(2)]
-
-        def scaled_from(dst, t, src):
-            nc.scalar.activation(out=dst, in_=src, func=ACT.Copy, scale=gain[:, t : t + 1])
-
-        def scaled(dst, t, cols):
-            scaled_from(dst, t, turned[t][:, cols])
-
-        def add_mates(t, cols, plain):
-            entries = lists["mate"][:, cols.start // 16 : cols.stop // 16]
-            nc.vector.tensor_tensor(out=sums[:, t, cols], in0=window[t][:].indirect(entries), in1=plain, op=ALU.add)
-
+        largest = [sb("largest%d" % t, [P, S], F32) for t in range(PACK)]
+        window = [sb("window%d" % t, [P, S], F32) for t in range(PACK)]
+        own = [sb("own%d" % t, [P, HALF], F32) for t in range(PACK)]
         halves = [slice(0, HALF), slice(HALF, S)]
         whole = slice(0, S)
-        scaled(window[0][:, halves[0]], 0, halves[0])
-        scaled(own_all[0][:, halves[0]], 0, halves[0])
-        for b in turned_late:
-            scaled_from(window[0][:, b * P : (b + 1) * P], 0, turned_late[b][:])
-            scaled_from(own_all[0][:, b * P : (b + 1) * P], 0, turned_late[b][:])
-        add_mates(0, whole, own_all[0][:])
-        scaled(window[1][:, whole], 1, whole)
-        scaled(own_all[1][:], 1, whole)
-        add_mates(1, whole, own_all[1][:])
-        for t in range(2, PACK):
-            scaled(window[t][:], t, slice(0, S))
-            scaled(own[t][0][:], t, halves[0])
-            add_mates(t, halves[0], own[t][0][:])
-        for t in range(2, PACK):
-            scaled(own[t][1][:], t, halves[1])
-            add_mates(t, halves[1], own[t][1][:])
+
+        def scaled(dst, t, cols):
+            nc.scalar.activation(out=dst, in_=largest[t][:, cols], func=ACT.Copy, scale=gain[:, t : t + 1])
+
+        for t in range(PACK):
+            first_layer_pass(e_acc[t], 1, t, "c1", True)
+            first_layer_pass(e_acc[t], 2, t, "c2", False)
+            nc.vector.tensor_tensor(out=largest[t][:], in0=e_acc[t][:], in1=relu_y[t][:], op=ALU.max)
+            scaled(window[t][:], t, whole)
+            scaled(own[t][:], t, halves[0])
+
+        sums = [sb("sums%d" % h, [P, PACK, HALF], F32) for h in range(2)]
+
+        def add_mates(t, cols, plain):
+            h = cols.start // HALF
+            part = slice(cols.start - h * HALF, cols.stop - h * HALF)
+            entries = lists["mate"][:, cols.start // 16 : cols.stop // 16]
+            nc.vector.tensor_tensor(
+                out=sums[h][:, t, part], in0=window[t][:].indirect(entries), in1=plain, op=ALU.add
+            )
 
         z_words = {}
         z_scales = {}
         z_bf = {}
 
-        def round_z(copy, c, tag=None):
-            z_bf[c] = sb("z_bf%d" % c, [P, PACK * CHUNK], BF16, tag=tag)
-            dst, src = interleaved(z_bf[c][:], sums[:, :, c * CHUNK : (c + 1) * CHUNK])
+        def round_z(copy, c):
+            z_bf[c] = sb("z_bf%d" % c, [P, PACK * CHUNK], BF16)
+            h, r = divmod(c, 2)
+            dst, src = interleaved(z_bf[c][:], sums[h][:, :, r * CHUNK : (r + 1) * CHUNK])
             copy(out=dst, in_=src)
 
         def quantise_z(c):
@@ -211,12 +188,22 @@ def tile_picked_charcnn_relu_po_kernel(
             z_scales[c] = sb("z_scales%d" % c, [P, CHUNK], U8)
             nc.vector.quantize_mx(out=z_words[c][:].bitcast(FP8X4), scales=z_scales[c][:], in_=z_bf[c][:])
 
-        round_z(nc.scalar.copy, 0)
-        round_z(nc.scalar.copy, 1)
-        round_z(nc.scalar.copy, 3)
-        quantise_z(0)
-        round_z(nc.vector.tensor_copy, 2, tag="z_bf0")
-        quantise_z(1)
+        chunks = [slice(c * CHUNK, (c + 1) * CHUNK) for c in range(S // CHUNK)]
+        for t in range(PACK):
+            add_mates(t, halves[0], own[t][:])
+        for t in range(2):
+            own_late = sb("own_late%d" % t, [P, HALF], F32)
+            scaled(own_late[:], t, halves[1])
+            add_mates(t, halves[1], own_late[:])
+        own_last = sb("own_last", [P, 2, 2, CHUNK], F32, tag="own3")
+        for r in range(2):
+            round_z(nc.scalar.copy, r)
+            quantise_z(r)
+            for t in range(2, PACK):
+                scaled(own_last[:, r, t - 2, :], t, chunks[2 + r])
+                add_mates(t, chunks[2 + r], own_last[:, r, t - 2, :])
+        round_z(nc.scalar.copy, 2)
+        round_z(nc.vector.tensor_copy, 3)
         quantise_z(2)
         quantise_z(3)
 
@@ -224,31 +211,31 @@ def tile_picked_charcnn_relu_po_kernel(
         out_words = out_1[0].rearrange("p n t -> p (n t)").bitcast(I32)
         y_scales = sb("y_scales", [P, S], U8)
         y_words = sb("y_words", [P, S], U32)
-        result_bf = [sb("result_bf%d" % h, [P, PACK * HALF], BF16) for h in range(2)]
-        for c in range(S // CHUNK):
-            acc = bank(4 + c, [P, PACK, CHUNK])
-            for t in range(PACK):
-                nc.tensor.matmul_mx(
-                    out=acc[:, t, :],
-                    lhsT=w3_codes[:, 2 * t * P : 2 * (t + 1) * P].bitcast(FP4X4),
-                    lhsT_scale=w3_plane[:, t * P : (t + 1) * P],
-                    rhs=z_words[c][:].bitcast(FP8X4),
-                    rhs_scale=z_scales[c][:],
-                    start=True,
-                    stop=True,
-                )
-            cols = slice(c * CHUNK, (c + 1) * CHUNK)
+        result_bf = sb("result_bf", [P, PACK * S], BF16)
+
+        def hand_on(cols):
+            wide = slice(PACK * cols.start, PACK * cols.stop)
+            nc.vector.quantize_mx(out=y_words[:, cols].bitcast(FP8X4), scales=y_scales[:, cols], in_=result_bf[:, wide])
+
+        for c, cols in enumerate(chunks):
             result = sb("result%d" % c, [P, PACK, CHUNK], F32)
-            nc.scalar.copy(out=result[:], in_=acc[:])
+            if c < 3:
+                acc = bank(c, [P, PACK, CHUNK])
+                for t in range(PACK):
+                    mx_pass(acc[:, t, :], 3, t, z_words[c][:], z_scales[c][:], True, True)
+                nc.scalar.copy(out=result[:], in_=acc[:])
+            else:
+                for pair, copy in enumerate((nc.scalar.copy, nc.vector.tensor_copy)):
+                    acc = bank(c + pair, [P, 2, CHUNK])
+                    for i in range(2):
+                        mx_pass(acc[:, i, :], 3, 2 * pair + i, z_words[c][:], z_scales[c][:], True, True)
+                    copy(out=result[:, 2 * pair : 2 * pair + 2, :], in_=acc[:])
             nc.sync.dma_start(out=out_rows[:, :, cols], in_=result[:])
-            h, r = divmod(c, 2)
-            dst, src = interleaved(result_bf[h][:, r * PACK * CHUNK : (r + 1) * PACK * CHUNK], result[:])
+            dst, src = interleaved(result_bf[:, c * PACK * CHUNK : (c + 1) * PACK * CHUNK], result[:])
             nc.vector.tensor_copy(out=dst, in_=src)
-            if r == 1:
-                nc.vector.quantize_mx(
-                    out=y_words[:, halves[h]].bitcast(FP8X4), scales=y_scales[:, halves[h]], in_=result_bf[h][:]
-                )
-        nc.sync.dma_start(out=out_words, in_=y_words[:].bitcast(I32))
+            if c % 2 == 1:
+                hand_on(halves[c // 2])
+                nc.sync.dma_start(out=out_words[:, halves[c // 2]], in_=y_words[:, halves[c // 2]].bitcast(I32))
         for q in range(QUADS):
             queue = nc.scalar if q % 2 else nc.sync
             queue.dma_start(out=out_2[0, 4 * q : 4 * q + 4, :].bitcast(I32), in_=y_scales[32 * q : 32 * q + 4, :].bitcast(I32))

@@ -56,8 +56,7 @@ def tile_picked_charcnn_relu_po_kernel(
         raw_codes = {w: sb("raw_codes%d" % w, [P, 2 * H], U8) for w in (1, 2, 3)}
         gain = sb("gain", [P, PACK], F32)
 
-        nc.vector.memset(x_plane[:, : T // 2].bitcast(I32), 0)
-        nc.gpsimd.memset(x_plane[:, T // 2 :].bitcast(I32), 0)
+        nc.vector.memset(x_plane[:].bitcast(I32), 0)
         for w in (2, 1, 3):
             nc.vector.memset(raw_plane[w][:].bitcast(I32), 0)
 
@@ -85,26 +84,24 @@ def tile_picked_charcnn_relu_po_kernel(
         load_codes(3, w3_words)
         load_scale_rows(raw_plane[3], w3_scales, range(QUADS))
 
-        codes = {}
-        plane = {}
+        codes = {w: sb("codes%d" % w, [P, 2 * H], U8) for w in (1, 2, 3)}
+        plane = {w: sb("plane%d" % w, [P, H], U8) for w in (1, 2, 3)}
 
-        def deal_codes(w):
-            codes[w] = sb("codes%d" % w, [P, 2 * H], U8)
+        def deal_codes(w, slots):
             nc.gpsimd.tensor_copy(
-                out=codes[w][:].rearrange("p (t m b) -> p t m b", t=PACK, b=2),
-                in_=raw_codes[w][:].rearrange("p (m t b) -> p t m b", t=PACK, b=2),
+                out=codes[w][:].rearrange("p (t m b) -> p t m b", t=PACK, b=2)[:, slots],
+                in_=raw_codes[w][:].rearrange("p (m t b) -> p t m b", t=PACK, b=2)[:, slots],
             )
 
-        def deal_plane(w):
-            plane[w] = sb("plane%d" % w, [P, H], U8)
+        def deal_plane(w, slots):
             nc.gpsimd.tensor_copy(
-                out=plane[w][:].rearrange("p (t m) -> p t m", t=PACK),
-                in_=raw_plane[w][:].rearrange("p (m t) -> p t m", t=PACK),
+                out=plane[w][:].rearrange("p (t m) -> p t m", t=PACK)[:, slots],
+                in_=raw_plane[w][:].rearrange("p (m t) -> p t m", t=PACK)[:, slots],
             )
 
-        for w in (2, 1, 3):
-            deal_codes(w)
-            deal_plane(w)
+        for w, slots in ((2, slice(0, 4)), (1, slice(0, 2)), (1, slice(2, 4)), (3, slice(0, 4))):
+            deal_codes(w, slots)
+            deal_plane(w, slots)
 
         picked_scales = {}
         picked_words = {}
@@ -140,11 +137,11 @@ def tile_picked_charcnn_relu_po_kernel(
 
         y_acc = [bank(t, [P, S]) for t in range(PACK)]
         e_acc = [bank(4 + t, [P, S]) for t in range(PACK)]
-        for t in range(PACK):
-            first_layer_pass(y_acc[t], 2, t, "c1", True)
         relu_y = [sb("relu_y%d" % t, [P, S], F32) for t in range(PACK)]
         for t in range(PACK):
-            first_layer_pass(y_acc[t], 1, t, "offs", False)
+            terms = [(2, "c1"), (1, "offs")]
+            for i, (w, name) in enumerate(terms if t < 2 else terms[::-1]):
+                first_layer_pass(y_acc[t], w, t, name, i == 0)
             nc.scalar.activation(out=relu_y[t][:], in_=y_acc[t][:], func=ACT.Relu)
 
         largest = [sb("largest%d" % t, [P, S], F32) for t in range(PACK)]
@@ -203,8 +200,8 @@ def tile_picked_charcnn_relu_po_kernel(
                 scaled(own_last[:, r, t - 2, :], t, chunks[2 + r])
                 add_mates(t, chunks[2 + r], own_last[:, r, t - 2, :])
         round_z(nc.scalar.copy, 2)
-        round_z(nc.vector.tensor_copy, 3)
         quantise_z(2)
+        round_z(nc.vector.tensor_copy, 3)
         quantise_z(3)
 
         out_rows = out_0.rearrange("(p t) j -> p t j", t=PACK)

@@ -214,25 +214,38 @@ def tile_picked_charcnn_relu_po_kernel(
             wide = slice(PACK * cols.start, PACK * cols.stop)
             nc.vector.quantize_mx(out=y_words[:, cols].bitcast(FP8X4), scales=y_scales[:, cols], in_=result_bf[:, wide])
 
-        for c, cols in enumerate(chunks):
-            result = sb("result%d" % c, [P, PACK, CHUNK], F32)
-            if c < 3:
-                acc = bank(c, [P, PACK, CHUNK])
-                for t in range(PACK):
-                    mx_pass(acc[:, t, :], 3, t, z_words[c][:], z_scales[c][:], True, True)
-                nc.scalar.copy(out=result[:], in_=acc[:])
-            else:
-                for pair, copy in enumerate((nc.scalar.copy, nc.vector.tensor_copy)):
-                    acc = bank(c + pair, [P, 2, CHUNK])
-                    for i in range(2):
-                        mx_pass(acc[:, i, :], 3, 2 * pair + i, z_words[c][:], z_scales[c][:], True, True)
-                    copy(out=result[:, 2 * pair : 2 * pair + 2, :], in_=acc[:])
-            nc.sync.dma_start(out=out_rows[:, :, cols], in_=result[:])
-            dst, src = interleaved(result_bf[:, c * PACK * CHUNK : (c + 1) * PACK * CHUNK], result[:])
+        result = [sb("result%d" % c, [P, PACK, CHUNK], F32) for c in range(S // CHUNK)]
+
+        def second_product(acc, c, slots):
+            for i, t in enumerate(slots):
+                mx_pass(acc[:, i, :], 3, t, z_words[c][:], z_scales[c][:], True, True)
+
+        def round_result(c):
+            dst, src = interleaved(result_bf[:, c * PACK * CHUNK : (c + 1) * PACK * CHUNK], result[c][:])
             nc.vector.tensor_copy(out=dst, in_=src)
-            if c % 2 == 1:
-                hand_on(halves[c // 2])
-                nc.sync.dma_start(out=out_words[:, halves[c // 2]], in_=y_words[:, halves[c // 2]].bitcast(I32))
+
+        def store_words(cols):
+            nc.sync.dma_start(out=out_words[:, cols], in_=y_words[:, cols].bitcast(I32))
+
+        for c in range(3):
+            acc = bank(c, [P, PACK, CHUNK])
+            second_product(acc, c, range(PACK))
+            nc.scalar.copy(out=result[c][:], in_=acc[:])
+            nc.sync.dma_start(out=out_rows[:, :, chunks[c]], in_=result[c][:])
+            if c < 2:
+                round_result(c)
+        hand_on(halves[0])
+        store_words(halves[0])
+        for pair, copy in enumerate((nc.vector.tensor_copy, nc.scalar.copy)):
+            acc = bank(3 + pair, [P, 2, CHUNK])
+            second_product(acc, 3, (2 * pair, 2 * pair + 1))
+            copy(out=result[3][:, 2 * pair : 2 * pair + 2, :], in_=acc[:])
+        nc.sync.dma_start(out=out_rows[:, :, chunks[3]], in_=result[3][:])
+        for c in (2, 3):
+            round_result(c)
+        for c in (2, 3):
+            hand_on(chunks[c])
+        store_words(halves[1])
         for q in range(QUADS):
             queue = nc.scalar if q % 2 else nc.sync
             queue.dma_start(out=out_2[0, 4 * q : 4 * q + 4, :].bitcast(I32), in_=y_scales[32 * q : 32 * q + 4, :].bitcast(I32))

@@ -224,9 +224,6 @@ def tile_picked_charcnn_relu_po_kernel(
             dst, src = interleaved(result_bf[:, c * PACK * CHUNK : (c + 1) * PACK * CHUNK], result[c][:])
             nc.vector.tensor_copy(out=dst, in_=src)
 
-        def store_words(cols):
-            nc.sync.dma_start(out=out_words[:, cols], in_=y_words[:, cols].bitcast(I32))
-
         for c in range(3):
             acc = bank(c, [P, PACK, CHUNK])
             second_product(acc, c, range(PACK))
@@ -235,7 +232,6 @@ def tile_picked_charcnn_relu_po_kernel(
             if c < 2:
                 round_result(c)
         hand_on(halves[0])
-        store_words(halves[0])
         for pair, copy in enumerate((nc.vector.tensor_copy, nc.scalar.copy)):
             acc = bank(3 + pair, [P, 2, CHUNK])
             second_product(acc, 3, (2 * pair, 2 * pair + 1))
@@ -245,7 +241,7 @@ def tile_picked_charcnn_relu_po_kernel(
             round_result(c)
         for c in (2, 3):
             hand_on(chunks[c])
-        store_words(halves[1])
+        nc.sync.dma_start(out=out_words, in_=y_words[:].bitcast(I32))
         for q in range(QUADS):
             queue = nc.scalar if q % 2 else nc.sync
             queue.dma_start(out=out_2[0, 4 * q : 4 * q + 4, :].bitcast(I32), in_=y_scales[32 * q : 32 * q + 4, :].bitcast(I32))

@@ -139,9 +139,9 @@ def tile_picked_charcnn_relu_po_kernel(
         e_acc = [bank(4 + t, [P, S]) for t in range(PACK)]
         relu_y = [sb("relu_y%d" % t, [P, S], F32) for t in range(PACK)]
         for t in range(PACK):
-            terms = [(2, "c1"), (1, "offs")]
-            for i, (w, name) in enumerate(terms if t < 2 else terms[::-1]):
-                first_layer_pass(y_acc[t], w, t, name, i == 0)
+            first_layer_pass(y_acc[t], 2, t, "c1", True)
+        for t in range(PACK):
+            first_layer_pass(y_acc[t], 1, t, "offs", False)
             nc.scalar.activation(out=relu_y[t][:], in_=y_acc[t][:], func=ACT.Relu)
 
         largest = [sb("largest%d" % t, [P, S], F32) for t in range(PACK)]

@@ -130,7 +130,23 @@ def tile_picked_charcnn_relu_po_kernel(
 
         gather_scales("c1")
         gather_scales("offs")
-        gather_words("c1")
+        picked_words["c1"] = sb("words_c1", [P, S], U32)
+        for h in range(2):
+            nc.vector.tensor_copy(
+                picked_words["c1"][:, h * HALF : (h + 1) * HALF],
+                x_table[:].bitcast(U32).indirect(lists["c1"][:, h * HALF // 16 : (h + 1) * HALF // 16]),
+            )
+            if h == 0:
+                for i, width in enumerate((S, HALF)):
+                    nc.tensor.matmul_mx(
+                        out=bank(6 + i, [P, width])[:],
+                        lhsT=picked_words["c1"][:, 0:P].bitcast(FP8X4),
+                        lhsT_scale=picked_scales["c1"][:, 0:P],
+                        rhs=codes[2][:, 0 : 2 * width].bitcast(FP4X4),
+                        rhs_scale=picked_scales["c1"][:, 0:width],
+                        start=True,
+                        stop=True,
+                    )
         gather_words("offs")
         gather_scales("c2")
         gather_words("c2")

@@ -160,65 +160,48 @@ def tile_picked_charcnn_relu_po_kernel(
             first_layer_pass(y_acc[t], 1, t, "offs", False)
             nc.scalar.activation(out=relu_y[t][:], in_=y_acc[t][:], func=ACT.Relu)
 
-        largest = [sb("largest%d" % t, [P, S], F32) for t in range(PACK)]
         window = [sb("window%d" % t, [P, S], F32) for t in range(PACK)]
-        own = [sb("own%d" % t, [P, HALF], F32) for t in range(PACK)]
         halves = [slice(0, HALF), slice(HALF, S)]
-        whole = slice(0, S)
-
-        def scaled(dst, t, cols):
-            nc.scalar.activation(out=dst, in_=largest[t][:, cols], func=ACT.Copy, scale=gain[:, t : t + 1])
+        chunks = [slice(c * CHUNK, (c + 1) * CHUNK) for c in range(S // CHUNK)]
 
         for t in range(PACK):
             first_layer_pass(e_acc[t], 1, t, "c1", True)
             first_layer_pass(e_acc[t], 2, t, "c2", False)
-            nc.vector.tensor_tensor(out=largest[t][:], in0=e_acc[t][:], in1=relu_y[t][:], op=ALU.max)
-            scaled(window[t][:], t, whole)
-            scaled(own[t][:], t, halves[0])
+            nc.vector.tensor_tensor(out=window[t][:], in0=e_acc[t][:], in1=relu_y[t][:], op=ALU.max)
 
+        mates = [sb("mates0", [P, PACK, HALF], F32), sb("mates1", [P, PACK, HALF], F32, tag="relu_y3")]
         sums = [sb("sums%d" % h, [P, PACK, HALF], F32) for h in range(2)]
-
-        def add_mates(t, cols, plain):
-            h = cols.start // HALF
-            part = slice(cols.start - h * HALF, cols.stop - h * HALF)
-            entries = lists["mate"][:, cols.start // 16 : cols.stop // 16]
-            nc.vector.tensor_tensor(
-                out=sums[h][:, t, part], in0=window[t][:].indirect(entries), in1=plain, op=ALU.add
-            )
-
         z_words = {}
         z_scales = {}
         z_bf = {}
 
-        def round_z(copy, c):
+        def fetch_mates(t, h):
+            entries = lists["mate"][:, h * HALF // 16 : (h + 1) * HALF // 16]
+            nc.scalar.activation(out=mates[h][:, t, :], in_=window[t][:].indirect(entries), func=ACT.Copy)
+
+        def add_mates(t, h):
+            nc.vector.tensor_tensor(out=sums[h][:, t, :], in0=window[t][:, halves[h]], in1=mates[h][:, t, :], op=ALU.add)
+
+        def round_z(c):
             z_bf[c] = sb("z_bf%d" % c, [P, PACK * CHUNK], BF16)
             h, r = divmod(c, 2)
             dst, src = interleaved(z_bf[c][:], sums[h][:, :, r * CHUNK : (r + 1) * CHUNK])
-            copy(out=dst, in_=src)
+            spread = gain[:].unsqueeze(1).unsqueeze(3).to_broadcast([P, CHUNK // 4, PACK, 4])
+            nc.vector.tensor_tensor(out=dst, in0=src, in1=spread, op=ALU.mult)
 
         def quantise_z(c):
             z_words[c] = sb("z_words%d" % c, [P, CHUNK], U32)
             z_scales[c] = sb("z_scales%d" % c, [P, CHUNK], U8)
             nc.vector.quantize_mx(out=z_words[c][:].bitcast(FP8X4), scales=z_scales[c][:], in_=z_bf[c][:])
 
-        chunks = [slice(c * CHUNK, (c + 1) * CHUNK) for c in range(S // CHUNK)]
-        for t in range(PACK):
-            add_mates(t, halves[0], own[t][:])
-        for t in range(2):
-            own_late = sb("own_late%d" % t, [P, HALF], F32)
-            scaled(own_late[:], t, halves[1])
-            add_mates(t, halves[1], own_late[:])
-        own_last = sb("own_last", [P, 2, 2, CHUNK], F32, tag="own3")
-        for r in range(2):
-            round_z(nc.scalar.copy, r)
-            quantise_z(r)
-            for t in range(2, PACK):
-                scaled(own_last[:, r, t - 2, :], t, chunks[2 + r])
-                add_mates(t, chunks[2 + r], own_last[:, r, t - 2, :])
-        round_z(nc.scalar.copy, 2)
-        quantise_z(2)
-        round_z(nc.vector.tensor_copy, 3)
-        quantise_z(3)
+        for h in range(2):
+            for t in range(PACK):
+                fetch_mates(t, h)
+                add_mates(t, h)
+            for c in (2 * h, 2 * h + 1):
+                round_z(c)
+            for c in (2 * h, 2 * h + 1):
+                quantise_z(c)
 
         out_rows = out_0.rearrange("(p t) j -> p t j", t=PACK)
         out_words = out_1[0].rearrange("p n t -> p (n t)").bitcast(I32)

@@ -171,9 +171,9 @@ def tile_picked_charcnn_relu_po_kernel(
 
         mates = [sb("mates0", [P, PACK, HALF], F32), sb("mates1", [P, PACK, HALF], F32, tag="relu_y3")]
         sums = [sb("sums%d" % h, [P, PACK, HALF], F32) for h in range(2)]
-        z_words = {}
-        z_scales = {}
-        z_bf = {}
+        z_bf = [sb("z_bf%d" % h, [P, PACK * HALF], BF16) for h in range(2)]
+        z_words = [sb("z_words%d" % h, [P, HALF], U32) for h in range(2)]
+        z_scales = [sb("z_scales%d" % h, [P, HALF], U8) for h in range(2)]
 
         def fetch_mates(t, h):
             entries = lists["mate"][:, h * HALF // 16 : (h + 1) * HALF // 16]
@@ -182,26 +182,32 @@ def tile_picked_charcnn_relu_po_kernel(
         def add_mates(t, h):
             nc.vector.tensor_tensor(out=sums[h][:, t, :], in0=window[t][:, halves[h]], in1=mates[h][:, t, :], op=ALU.add)
 
-        def round_z(c):
-            z_bf[c] = sb("z_bf%d" % c, [P, PACK * CHUNK], BF16)
-            h, r = divmod(c, 2)
-            dst, src = interleaved(z_bf[c][:], sums[h][:, :, r * CHUNK : (r + 1) * CHUNK])
-            spread = gain[:].unsqueeze(1).unsqueeze(3).to_broadcast([P, CHUNK // 4, PACK, 4])
+        def round_z(h, cols):
+            dst, src = interleaved(z_bf[h][:, PACK * cols.start : PACK * cols.stop], sums[h][:, :, cols])
+            spread = gain[:].unsqueeze(1).unsqueeze(3).to_broadcast([P, (cols.stop - cols.start) // 4, PACK, 4])
             nc.vector.tensor_tensor(out=dst, in0=src, in1=spread, op=ALU.mult)
 
-        def quantise_z(c):
-            z_words[c] = sb("z_words%d" % c, [P, CHUNK], U32)
-            z_scales[c] = sb("z_scales%d" % c, [P, CHUNK], U8)
-            nc.vector.quantize_mx(out=z_words[c][:].bitcast(FP8X4), scales=z_scales[c][:], in_=z_bf[c][:])
+        def quantise_z(h, cols):
+            nc.vector.quantize_mx(
+                out=z_words[h][:, cols].bitcast(FP8X4),
+                scales=z_scales[h][:, cols],
+                in_=z_bf[h][:, PACK * cols.start : PACK * cols.stop],
+            )
 
         for h in range(2):
             for t in range(PACK):
                 fetch_mates(t, h)
-                add_mates(t, h)
-            for c in (2 * h, 2 * h + 1):
-                round_z(c)
-            for c in (2 * h, 2 * h + 1):
-                quantise_z(c)
+        for t in range(PACK):
+            add_mates(t, 0)
+        add_mates(0, 1)
+        round_z(0, halves[0])
+        add_mates(1, 1)
+        quantise_z(0, halves[0])
+        add_mates(2, 1)
+        add_mates(3, 1)
+        for step in (round_z, quantise_z):
+            for cols in chunks[:2]:
+                step(1, cols)
 
         out_rows = out_0.rearrange("(p t) j -> p t j", t=PACK)
         out_words = out_1[0].rearrange("p n t -> p (n t)").bitcast(I32)
@@ -217,7 +223,7 @@ def tile_picked_charcnn_relu_po_kernel(
 
         def second_product(acc, c, slots):
             for i, t in enumerate(slots):
-                mx_pass(acc[:, i, :], 3, t, z_words[c][:], z_scales[c][:], True, True)
+                mx_pass(acc[:, i, :], 3, t, z_words[c // 2][:, chunks[c % 2]], z_scales[c // 2][:, chunks[c % 2]], True, True)
 
         def round_result(c):
             dst, src = interleaved(result_bf[:, c * PACK * CHUNK : (c + 1) * PACK * CHUNK], result[c][:])
@@ -229,7 +235,10 @@ def tile_picked_charcnn_relu_po_kernel(
             nc.scalar.copy(out=result[c][:], in_=acc[:])
             nc.sync.dma_start(out=out_rows[:, :, chunks[c]], in_=result[c][:])
             if c < 2:
-                round_result(c)
+                nc.scalar.copy(
+                    out=result_bf[:, c * PACK * CHUNK : (c + 1) * PACK * CHUNK].rearrange("p (j t) -> p j t", t=PACK),
+                    in_=acc[:].rearrange("p t j -> p j t"),
+                )
         hand_on(halves[0])
         for pair, copy in enumerate((nc.vector.tensor_copy, nc.scalar.copy)):
             acc = bank(3 + pair, [P, 2, CHUNK])

@@ -177,7 +177,10 @@ def tile_picked_charcnn_relu_po_kernel(
 
         def fetch_mates(t, h):
             entries = lists["mate"][:, h * HALF // 16 : (h + 1) * HALF // 16]
-            nc.scalar.activation(out=mates[h][:, t, :], in_=window[t][:].indirect(entries), func=ACT.Copy)
+            if (t, h) == (2, 0):
+                nc.vector.tensor_copy(mates[h][:, t, :], window[t][:].indirect(entries))
+            else:
+                nc.scalar.activation(out=mates[h][:, t, :], in_=window[t][:].indirect(entries), func=ACT.Copy)
 
         def add_mates(t, h):
             nc.vector.tensor_tensor(out=sums[h][:, t, :], in0=window[t][:, halves[h]], in1=mates[h][:, t, :], op=ALU.add)
@@ -213,38 +216,38 @@ def tile_picked_charcnn_relu_po_kernel(
         out_words = out_1[0].rearrange("p n t -> p (n t)").bitcast(I32)
         y_scales = sb("y_scales", [P, S], U8)
         y_words = sb("y_words", [P, S], U32)
-        result_bf = sb("result_bf", [P, PACK * S], BF16)
+        result_bf = sb("result_bf", [P, PACK * S], BF16, tag="z_bf1")
 
         def hand_on(cols):
             wide = slice(PACK * cols.start, PACK * cols.stop)
             nc.vector.quantize_mx(out=y_words[:, cols].bitcast(FP8X4), scales=y_scales[:, cols], in_=result_bf[:, wide])
 
-        result = [sb("result%d" % c, [P, PACK, CHUNK], F32) for c in range(S // CHUNK)]
+        first = sb("first", [P, 2, PACK, CHUNK], F32)
+        result = [first[:, 0], first[:, 1]] + [sb("result%d" % c, [P, PACK, CHUNK], F32)[:] for c in (2, 3)]
 
         def second_product(acc, c, slots):
             for i, t in enumerate(slots):
                 mx_pass(acc[:, i, :], 3, t, z_words[c // 2][:, chunks[c % 2]], z_scales[c // 2][:, chunks[c % 2]], True, True)
 
         def round_result(c):
-            dst, src = interleaved(result_bf[:, c * PACK * CHUNK : (c + 1) * PACK * CHUNK], result[c][:])
+            dst, src = interleaved(result_bf[:, c * PACK * CHUNK : (c + 1) * PACK * CHUNK], result[c])
             nc.vector.tensor_copy(out=dst, in_=src)
 
         for c in range(3):
             acc = bank(c, [P, PACK, CHUNK])
             second_product(acc, c, range(PACK))
-            nc.scalar.copy(out=result[c][:], in_=acc[:])
-            nc.sync.dma_start(out=out_rows[:, :, chunks[c]], in_=result[c][:])
-            if c < 2:
-                nc.scalar.copy(
-                    out=result_bf[:, c * PACK * CHUNK : (c + 1) * PACK * CHUNK].rearrange("p (j t) -> p j t", t=PACK),
-                    in_=acc[:].rearrange("p t j -> p j t"),
-                )
-        hand_on(halves[0])
+            nc.scalar.copy(out=result[c], in_=acc[:])
+            nc.sync.dma_start(out=out_rows[:, :, chunks[c]], in_=result[c])
+        nc.vector.tensor_copy(
+            out=result_bf[:, 0 : PACK * HALF].rearrange("p (b c i t) -> p b c t i", b=2, i=4, t=PACK),
+            in_=first[:].rearrange("p b t (c i) -> p b c t i", i=4),
+        )
         for pair, copy in enumerate((nc.vector.tensor_copy, nc.scalar.copy)):
             acc = bank(3 + pair, [P, 2, CHUNK])
             second_product(acc, 3, (2 * pair, 2 * pair + 1))
             copy(out=result[3][:, 2 * pair : 2 * pair + 2, :], in_=acc[:])
-        nc.sync.dma_start(out=out_rows[:, :, chunks[3]], in_=result[3][:])
+        nc.sync.dma_start(out=out_rows[:, :, chunks[3]], in_=result[3])
+        hand_on(halves[0])
         for c in (2, 3):
             round_result(c)
         for c in (2, 3):

@@ -136,17 +136,6 @@ def tile_picked_charcnn_relu_po_kernel(
                 picked_words["c1"][:, h * HALF : (h + 1) * HALF],
                 x_table[:].bitcast(U32).indirect(lists["c1"][:, h * HALF // 16 : (h + 1) * HALF // 16]),
             )
-            if h == 0:
-                for i, width in enumerate((S, HALF)):
-                    nc.tensor.matmul_mx(
-                        out=bank(6 + i, [P, width])[:],
-                        lhsT=picked_words["c1"][:, 0:P].bitcast(FP8X4),
-                        lhsT_scale=picked_scales["c1"][:, 0:P],
-                        rhs=codes[2][:, 0 : 2 * width].bitcast(FP4X4),
-                        rhs_scale=picked_scales["c1"][:, 0:width],
-                        start=True,
-                        stop=True,
-                    )
         gather_words("offs")
         gather_scales("c2")
         gather_words("c2")

@@ -22,6 +22,7 @@ QUADS = 4
 HALF = S // 2
 CHUNK = 128
 LIST_COLS = S // 16
+PAIR_BYTES = 2 * S * 4
 
 
 def interleaved(dst, src):
@@ -38,6 +39,7 @@ def tile_picked_charcnn_relu_po_kernel(
     nc = tc.nc
     with ExitStack() as ctx:
         held = ctx.enter_context(tc.tile_pool(name="held", bufs=1))
+        placed = ctx.enter_context(tc.tile_pool(name="placed", bufs=1))
         psum = ctx.enter_context(tc.psum_pool(name="psum", bufs=1))
 
         def sb(name, shape, dtype, tag=None):
@@ -52,7 +54,8 @@ def tile_picked_charcnn_relu_po_kernel(
 
         x_plane = sb("x_plane", [P, T], U8)
         x_table = sb("x_table", [P, T], I32)
-        raw_plane = {w: sb("raw_plane%d" % w, [P, H], U8) for w in (1, 2, 3)}
+        raw_plane = {w: sb("raw_plane%d" % w, [P, H], U8) for w in (1, 2)}
+        raw_plane[3] = placed.tile([P, H], U8, name="raw_plane3", offset=PAIR_BYTES - H // 2)
         raw_codes = {w: sb("raw_codes%d" % w, [P, 2 * H], U8) for w in (1, 2, 3)}
         gain = sb("gain", [P, PACK], F32)
 
@@ -88,9 +91,9 @@ def tile_picked_charcnn_relu_po_kernel(
         plane = {w: sb("plane%d" % w, [P, H], U8) for w in (1, 2, 3)}
 
         def deal_codes(w, slots):
-            nc.gpsimd.tensor_copy(
-                out=codes[w][:].rearrange("p (t m b) -> p t m b", t=PACK, b=2)[:, slots],
-                in_=raw_codes[w][:].rearrange("p (m t b) -> p t m b", t=PACK, b=2)[:, slots],
+            nc.scalar.copy(
+                out=codes[w][:].bitcast(U16).rearrange("p (t m) -> p t m", t=PACK)[:, slots],
+                in_=raw_codes[w][:].bitcast(U16).rearrange("p (m t) -> p t m", t=PACK)[:, slots],
             )
 
         def deal_plane(w, slots):
@@ -99,9 +102,14 @@ def tile_picked_charcnn_relu_po_kernel(
                 in_=raw_plane[w][:].rearrange("p (m t) -> p t m", t=PACK)[:, slots],
             )
 
-        for w, slots in ((2, slice(0, 4)), (1, slice(0, 2)), (1, slice(2, 4)), (3, slice(0, 4))):
-            deal_codes(w, slots)
+        for w in (2, 1):
+            deal_codes(w, slice(0, PACK))
+        for w, slots in ((2, slice(1, 4, 2)), (2, slice(0, 4, 2)), (1, slice(1, 4, 2)), (1, slice(0, 4, 2)), (3, slice(0, 4))):
             deal_plane(w, slots)
+        nc.gpsimd.tensor_copy(
+            out=codes[3][:].rearrange("p (t m b) -> p t m b", t=PACK, b=2),
+            in_=raw_codes[3][:].rearrange("p (m t b) -> p t m b", t=PACK, b=2),
+        )
 
         picked_scales = {}
         picked_words = {}
@@ -140,26 +148,41 @@ def tile_picked_charcnn_relu_po_kernel(
         gather_scales("c2")
         gather_words("c2")
 
+        gain_size = sb("gain_size", [P, PACK], F32)
+        gain_sign = sb("gain_sign", [P, PACK], BF16)
+        nc.scalar.activation(out=gain_size[:], in_=gain[:], func=ACT.Abs)
+        nc.scalar.activation(out=gain_sign[:], in_=gain[:], func=ACT.Sign)
+
+        order = (1, 3, 0, 2)
         y_acc = [bank(t, [P, S]) for t in range(PACK)]
         e_acc = [bank(4 + t, [P, S]) for t in range(PACK)]
         relu_y = [sb("relu_y%d" % t, [P, S], F32) for t in range(PACK)]
-        for t in range(PACK):
-            first_layer_pass(y_acc[t], 2, t, "c1", True)
-        for t in range(PACK):
+        for h in range(2):
+            cols = slice(h * HALF, (h + 1) * HALF)
+            for t in order:
+                mx_pass(y_acc[t][:, cols], 2, t, picked_words["c1"][:, cols], picked_scales["c1"][:, cols], h == 0, False)
+        for t in order:
             first_layer_pass(y_acc[t], 1, t, "offs", False)
-            nc.scalar.activation(out=relu_y[t][:], in_=y_acc[t][:], func=ACT.Relu)
+            nc.scalar.activation(out=relu_y[t][:], in_=y_acc[t][:], func=ACT.Relu, scale=gain_size[:, t : t + 1])
 
-        window = [sb("window%d" % t, [P, S], F32) for t in range(PACK)]
+        pair = [placed.tile([P, 2 * S], F32, name="pair%d" % u, offset=u * PAIR_BYTES) for u in range(2)]
+        odd = [sb("odd%d" % u, [P, S], F32) for u in range(2)]
+        window = [pair[0], odd[0], pair[1], odd[1]]
         halves = [slice(0, HALF), slice(HALF, S)]
         chunks = [slice(c * CHUNK, (c + 1) * CHUNK) for c in range(S // CHUNK)]
 
-        for t in range(PACK):
+        for t in order:
             first_layer_pass(e_acc[t], 1, t, "c1", True)
             first_layer_pass(e_acc[t], 2, t, "c2", False)
-            nc.vector.tensor_tensor(out=window[t][:], in0=e_acc[t][:], in1=relu_y[t][:], op=ALU.max)
+            nc.vector.scalar_tensor_tensor(
+                out=window[t][:, 0:S], in0=e_acc[t][:], scalar=gain_size[:, t : t + 1], in1=relu_y[t][:],
+                op0=ALU.mult, op1=ALU.max,
+            )
+            if t % 2:
+                nc.gpsimd.tensor_copy(out=pair[t // 2][:, S : 2 * S], in_=odd[t // 2][:])
 
-        mates = [sb("mates0", [P, PACK, HALF], F32), sb("mates1", [P, PACK, HALF], F32, tag="relu_y3")]
-        sums = [sb("sums%d" % h, [P, PACK, HALF], F32) for h in range(2)]
+        mates = [sb("mates0", [P, PACK, HALF], F32), sb("mates1", [P, PACK, HALF], F32, tag="relu_y2")]
+        sums = [sb("sums0", [P, 2, 2 * HALF], BF16), sb("sums1", [P, 2, 2 * HALF], BF16, tag="mates0")]
         z_bf = [sb("z_bf%d" % h, [P, PACK * HALF], BF16) for h in range(2)]
         z_words = [sb("z_words%d" % h, [P, HALF], U32) for h in range(2)]
         z_scales = [sb("z_scales%d" % h, [P, HALF], U8) for h in range(2)]
@@ -171,13 +194,23 @@ def tile_picked_charcnn_relu_po_kernel(
             else:
                 nc.scalar.activation(out=mates[h][:, t, :], in_=window[t][:].indirect(entries), func=ACT.Copy)
 
-        def add_mates(t, h):
-            nc.vector.tensor_tensor(out=sums[h][:, t, :], in0=window[t][:, halves[h]], in1=mates[h][:, t, :], op=ALU.add)
+        def add_mates(u, h):
+            own = pair[u][:].rearrange("p (e j) -> p e j", e=2)[:, :, halves[h]]
+            nc.vector.tensor_tensor(
+                out=sums[h][:, u, :].rearrange("p (c i e) -> p c e i", i=4, e=2),
+                in0=own.rearrange("p e (c i) -> p c e i", i=4),
+                in1=mates[h][:, 2 * u : 2 * u + 2, :].rearrange("p e (c i) -> p c e i", i=4),
+                op=ALU.add,
+            )
 
-        def round_z(h, cols):
-            dst, src = interleaved(z_bf[h][:, PACK * cols.start : PACK * cols.stop], sums[h][:, :, cols])
-            spread = gain[:].unsqueeze(1).unsqueeze(3).to_broadcast([P, (cols.stop - cols.start) // 4, PACK, 4])
-            nc.vector.tensor_tensor(out=dst, in0=src, in1=spread, op=ALU.mult)
+        def sign_z(h, cols):
+            width = cols.stop - cols.start
+            nc.vector.tensor_tensor(
+                out=z_bf[h][:, PACK * cols.start : PACK * cols.stop].rearrange("p (j u e) -> p j u e", u=2, e=2),
+                in0=sums[h][:, :, 2 * cols.start : 2 * cols.stop].rearrange("p u (j e) -> p j u e", e=2),
+                in1=gain_sign[:].rearrange("p (u e) -> p u e", e=2).unsqueeze(1).to_broadcast([P, width, 2, 2]),
+                op=ALU.mult,
+            )
 
         def quantise_z(h, cols):
             nc.vector.quantize_mx(
@@ -186,18 +219,17 @@ def tile_picked_charcnn_relu_po_kernel(
                 in_=z_bf[h][:, PACK * cols.start : PACK * cols.stop],
             )
 
-        for h in range(2):
-            for t in range(PACK):
-                fetch_mates(t, h)
-        for t in range(PACK):
-            add_mates(t, 0)
+        for t in order:
+            fetch_mates(t, 0)
+        for t in (1, 0, 3, 2):
+            fetch_mates(t, 1)
+        add_mates(0, 0)
+        add_mates(1, 0)
+        sign_z(0, halves[0])
         add_mates(0, 1)
-        round_z(0, halves[0])
-        add_mates(1, 1)
         quantise_z(0, halves[0])
-        add_mates(2, 1)
-        add_mates(3, 1)
-        for step in (round_z, quantise_z):
+        add_mates(1, 1)
+        for step in (sign_z, quantise_z):
             for cols in chunks[:2]:
                 step(1, cols)
 
@@ -231,10 +263,10 @@ def tile_picked_charcnn_relu_po_kernel(
             out=result_bf[:, 0 : PACK * HALF].rearrange("p (b c i t) -> p b c t i", b=2, i=4, t=PACK),
             in_=first[:].rearrange("p b t (c i) -> p b c t i", i=4),
         )
-        for pair, copy in enumerate((nc.vector.tensor_copy, nc.scalar.copy)):
-            acc = bank(3 + pair, [P, 2, CHUNK])
-            second_product(acc, 3, (2 * pair, 2 * pair + 1))
-            copy(out=result[3][:, 2 * pair : 2 * pair + 2, :], in_=acc[:])
+        for duo, copy in enumerate((nc.vector.tensor_copy, nc.scalar.copy)):
+            acc = bank(3 + duo, [P, 2, CHUNK])
+            second_product(acc, 3, (2 * duo, 2 * duo + 1))
+            copy(out=result[3][:, 2 * duo : 2 * duo + 2, :], in_=acc[:])
         nc.sync.dma_start(out=out_rows[:, :, chunks[3]], in_=result[3])
         hand_on(halves[0])
         for c in (2, 3):

@@ -182,24 +182,24 @@ def tile_picked_charcnn_relu_po_kernel(
                 nc.gpsimd.tensor_copy(out=pair[t // 2][:, S : 2 * S], in_=odd[t // 2][:])
 
         mates = [sb("mates0", [P, PACK, HALF], F32), sb("mates1", [P, PACK, HALF], F32, tag="relu_y2")]
-        sums = [sb("sums0", [P, 2, 2 * HALF], BF16), sb("sums1", [P, 2, 2 * HALF], BF16, tag="mates0")]
+        sums = [sb("sums%d" % h, [P, 2, 2 * HALF], BF16) for h in range(2)]
         z_bf = [sb("z_bf%d" % h, [P, PACK * HALF], BF16) for h in range(2)]
         z_words = [sb("z_words%d" % h, [P, HALF], U32) for h in range(2)]
         z_scales = [sb("z_scales%d" % h, [P, HALF], U8) for h in range(2)]
 
         def fetch_mates(t, h):
             entries = lists["mate"][:, h * HALF // 16 : (h + 1) * HALF // 16]
-            if (t, h) == (2, 0):
+            if h == 0 and t % 2 == 0:
                 nc.vector.tensor_copy(mates[h][:, t, :], window[t][:].indirect(entries))
             else:
                 nc.scalar.activation(out=mates[h][:, t, :], in_=window[t][:].indirect(entries), func=ACT.Copy)
 
-        def add_mates(u, h):
-            own = pair[u][:].rearrange("p (e j) -> p e j", e=2)[:, :, halves[h]]
+        def add_mates(u, h, cols):
+            own = pair[u][:].rearrange("p (e j) -> p e j", e=2)[:, :, h * HALF + cols.start : h * HALF + cols.stop]
             nc.vector.tensor_tensor(
-                out=sums[h][:, u, :].rearrange("p (c i e) -> p c e i", i=4, e=2),
+                out=sums[h][:, u, 2 * cols.start : 2 * cols.stop].rearrange("p (c i e) -> p c e i", i=4, e=2),
                 in0=own.rearrange("p e (c i) -> p c e i", i=4),
-                in1=mates[h][:, 2 * u : 2 * u + 2, :].rearrange("p e (c i) -> p c e i", i=4),
+                in1=mates[h][:, 2 * u : 2 * u + 2, cols].rearrange("p e (c i) -> p c e i", i=4),
                 op=ALU.add,
             )
 
@@ -223,12 +223,14 @@ def tile_picked_charcnn_relu_po_kernel(
             fetch_mates(t, 0)
         for t in (1, 0, 3, 2):
             fetch_mates(t, 1)
-        add_mates(0, 0)
-        add_mates(1, 0)
-        sign_z(0, halves[0])
-        add_mates(0, 1)
-        quantise_z(0, halves[0])
-        add_mates(1, 1)
+        add_mates(0, 0, halves[0])
+        add_mates(1, 0, halves[0])
+        add_mates(0, 1, halves[0])
+        for step in (sign_z, quantise_z):
+            for cols in chunks[:2]:
+                step(0, cols)
+        for cols in chunks[:2]:
+            add_mates(1, 1, cols)
         for step in (sign_z, quantise_z):
             for cols in chunks[:2]:
                 step(1, cols)

@@ -271,11 +271,12 @@ def tile_picked_charcnn_relu_po_kernel(
             copy(out=result[3][:, 2 * duo : 2 * duo + 2, :], in_=acc[:])
         nc.sync.dma_start(out=out_rows[:, :, chunks[3]], in_=result[3])
         hand_on(halves[0])
+        nc.sync.dma_start(out=out_words[:, halves[0]], in_=y_words[:, halves[0]].bitcast(I32))
         for c in (2, 3):
             round_result(c)
         for c in (2, 3):
             hand_on(chunks[c])
-        nc.sync.dma_start(out=out_words, in_=y_words[:].bitcast(I32))
+        nc.sync.dma_start(out=out_words[:, halves[1]], in_=y_words[:, halves[1]].bitcast(I32))
         for q in range(QUADS):
             queue = nc.scalar if q % 2 else nc.sync
             queue.dma_start(out=out_2[0, 4 * q : 4 * q + 4, :].bitcast(I32), in_=y_scales[32 * q : 32 * q + 4, :].bitcast(I32))

@@ -102,9 +102,19 @@ def tile_picked_charcnn_relu_po_kernel(
                 in_=raw_plane[w][:].rearrange("p (m t) -> p t m", t=PACK)[:, slots],
             )
 
+        warm_bf = sb("warm_bf", [P, PACK * P], BF16)
+        warm_words = sb("warm_words", [P, P], U32)
+        warm_scales = sb("warm_scales", [P, P], U8)
+        nc.scalar.activation(
+            out=warm_bf[:].rearrange("p (a n) -> p a n", a=2),
+            in_=raw_codes[2][:].bitcast(U32).unsqueeze(1).to_broadcast([P, 2, 2 * P]),
+            func=ACT.Copy,
+        )
+        nc.vector.quantize_mx(out=warm_words[:].bitcast(FP8X4), scales=warm_scales[:], in_=warm_bf[:])
+
         for w in (2, 1):
             deal_codes(w, slice(0, PACK))
-        for w, slots in ((2, slice(1, 4, 2)), (2, slice(0, 4, 2)), (1, slice(1, 4, 2)), (1, slice(0, 4, 2)), (3, slice(0, 4))):
+        for w, slots in ((2, slice(1, 4, 2)), (2, slice(0, 4, 2)), (1, slice(0, 4)), (3, slice(0, 4))):
             deal_plane(w, slots)
         nc.gpsimd.tensor_copy(
             out=codes[3][:].rearrange("p (t m b) -> p t m b", t=PACK, b=2),
@@ -122,6 +132,12 @@ def tile_picked_charcnn_relu_po_kernel(
             picked_words[name] = sb("words_" + name, [P, S], U32)
             nc.vector.tensor_copy(picked_words[name][:], x_table[:].bitcast(U32).indirect(lists[name][:]))
 
+        def gather_half(picked, name, table, h):
+            nc.vector.tensor_copy(
+                picked[name][:, h * HALF : (h + 1) * HALF],
+                table.indirect(lists[name][:, h * HALF // 16 : (h + 1) * HALF // 16]),
+            )
+
         def mx_pass(acc, w, t, words, scales, start, stop):
             nc.tensor.matmul_mx(
                 out=acc,
@@ -137,16 +153,27 @@ def tile_picked_charcnn_relu_po_kernel(
             mx_pass(acc[:], w, t, picked_words[name][:], picked_scales[name][:], start, not start)
 
         gather_scales("c1")
+        warm_acc = bank(7, [P, S])
+        for n in range(2):
+            nc.tensor.matmul_mx(
+                out=warm_acc[:],
+                lhsT=warm_words[:].bitcast(FP8X4),
+                lhsT_scale=warm_scales[:],
+                rhs=raw_codes[2][:].bitcast(FP4X4),
+                rhs_scale=picked_scales["c1"][:],
+                start=True,
+                stop=True,
+            )
         gather_scales("offs")
         picked_words["c1"] = sb("words_c1", [P, S], U32)
         for h in range(2):
-            nc.vector.tensor_copy(
-                picked_words["c1"][:, h * HALF : (h + 1) * HALF],
-                x_table[:].bitcast(U32).indirect(lists["c1"][:, h * HALF // 16 : (h + 1) * HALF // 16]),
-            )
+            gather_half(picked_words, "c1", x_table[:].bitcast(U32), h)
         gather_words("offs")
-        gather_scales("c2")
-        gather_words("c2")
+        picked_scales["c2"] = sb("scales_c2", [P, S], U8)
+        picked_words["c2"] = sb("words_c2", [P, S], U32)
+        for h in range(2):
+            gather_half(picked_scales, "c2", x_plane[:], h)
+            gather_half(picked_words, "c2", x_table[:].bitcast(U32), h)
 
         gain_size = sb("gain_size", [P, PACK], F32)
         gain_sign = sb("gain_sign", [P, PACK], BF16)
@@ -155,7 +182,6 @@ def tile_picked_charcnn_relu_po_kernel(
 
         order = (1, 3, 0, 2)
         y_acc = [bank(t, [P, S]) for t in range(PACK)]
-        e_acc = [bank(4 + t, [P, S]) for t in range(PACK)]
         relu_y = [sb("relu_y%d" % t, [P, S], F32) for t in range(PACK)]
         for h in range(2):
             cols = slice(h * HALF, (h + 1) * HALF)
@@ -171,15 +197,24 @@ def tile_picked_charcnn_relu_po_kernel(
         halves = [slice(0, HALF), slice(HALF, S)]
         chunks = [slice(c * CHUNK, (c + 1) * CHUNK) for c in range(S // CHUNK)]
 
-        for t in order:
-            first_layer_pass(e_acc[t], 1, t, "c1", True)
-            first_layer_pass(e_acc[t], 2, t, "c2", False)
-            nc.vector.scalar_tensor_tensor(
-                out=window[t][:, 0:S], in0=e_acc[t][:], scalar=gain_size[:, t : t + 1], in1=relu_y[t][:],
-                op0=ALU.mult, op1=ALU.max,
-            )
-            if t % 2:
-                nc.gpsimd.tensor_copy(out=pair[t // 2][:, S : 2 * S], in_=odd[t // 2][:])
+        for h in range(2):
+            cols = halves[h]
+            for group in range(2):
+                slots = order[2 * group : 2 * group + 2]
+                e_acc = bank(4 + 2 * h + group, [P, 2, HALF])
+                for w, name in ((1, "c1"), (2, "c2")):
+                    for i, t in enumerate(slots):
+                        mx_pass(
+                            e_acc[:, i, :], w, t, picked_words[name][:, cols], picked_scales[name][:, cols],
+                            (w, i) == (1, 0), (w, i) == (2, 1),
+                        )
+                for i, t in enumerate(slots):
+                    nc.vector.scalar_tensor_tensor(
+                        out=window[t][:, cols], in0=e_acc[:, i, :], scalar=gain_size[:, t : t + 1],
+                        in1=relu_y[t][:, cols], op0=ALU.mult, op1=ALU.max,
+                    )
+                    if h == 1 and t % 2:
+                        nc.gpsimd.tensor_copy(out=pair[t // 2][:, S : 2 * S], in_=odd[t // 2][:])
 
         mates = [sb("mates0", [P, PACK, HALF], F32), sb("mates1", [P, PACK, HALF], F32, tag="relu_y2")]
         sums = [sb("sums%d" % h, [P, 2, 2 * HALF], BF16) for h in range(2)]

@@ -105,10 +105,9 @@ def tile_picked_charcnn_relu_po_kernel(
         warm_bf = sb("warm_bf", [P, PACK * P], BF16)
         warm_words = sb("warm_words", [P, P], U32)
         warm_scales = sb("warm_scales", [P, P], U8)
-        nc.scalar.activation(
+        nc.vector.tensor_copy(
             out=warm_bf[:].rearrange("p (a n) -> p a n", a=2),
-            in_=raw_codes[2][:].bitcast(U32).unsqueeze(1).to_broadcast([P, 2, 2 * P]),
-            func=ACT.Copy,
+            in_=raw_codes[2][:].bitcast(I32).unsqueeze(1).to_broadcast([P, 2, 2 * P]),
         )
         nc.vector.quantize_mx(out=warm_words[:].bitcast(FP8X4), scales=warm_scales[:], in_=warm_bf[:])
 

@@ -257,12 +257,15 @@ def tile_picked_charcnn_relu_po_kernel(
             fetch_mates(t, 0)
         for t in (1, 0, 3, 2):
             fetch_mates(t, 1)
-        add_mates(0, 0, halves[0])
-        add_mates(1, 0, halves[0])
+        add_mates(0, 0, chunks[0])
+        add_mates(1, 0, chunks[0])
+        add_mates(0, 0, chunks[1])
+        sign_z(0, chunks[0])
+        add_mates(1, 0, chunks[1])
+        quantise_z(0, chunks[0])
+        sign_z(0, chunks[1])
         add_mates(0, 1, halves[0])
-        for step in (sign_z, quantise_z):
-            for cols in chunks[:2]:
-                step(0, cols)
+        quantise_z(0, chunks[1])
         for cols in chunks[:2]:
             add_mates(1, 1, cols)
         for step in (sign_z, quantise_z):

from contextlib import ExitStack

import concourse.mybir as mybir

K, T, S, H, N = 512, 2048, 512, 512, 512
FLOPS = 2 * (4 * K * H * S + H * N * S)

F32 = mybir.dt.float32
BF16 = mybir.dt.bfloat16
I32 = mybir.dt.int32
U32 = mybir.dt.uint32
U16 = mybir.dt.uint16
U8 = mybir.dt.uint8
FP8X4 = mybir.dt.float8_e4m3fn_x4
FP4X4 = mybir.dt.float4_e2m1fn_x4
ALU = mybir.AluOpType
ACT = mybir.ActivationFunctionType

P = 128
PACK = 4
QUADS = 4
HALF = S // 2
CHUNK = 128
LIST_COLS = S // 16
PAIR_BYTES = 2 * S * 4


def interleaved(dst, src):
    return (
        dst.rearrange("p (c i t) -> p c t i", i=4, t=PACK),
        src.rearrange("p t (c i) -> p c t i", i=4),
    )


def tile_picked_charcnn_relu_po_kernel(
    tc, x_words, x_scales, w1_words, w1_scales, w2_words, w2_scales, gn, w3_words, w3_scales,
    offs, c1, c2, mate, out_0, out_1, out_2,
):
    nc = tc.nc
    with ExitStack() as ctx:
        held = ctx.enter_context(tc.tile_pool(name="held", bufs=1))
        placed = ctx.enter_context(tc.tile_pool(name="placed", bufs=1))
        psum = ctx.enter_context(tc.psum_pool(name="psum", bufs=1))

        def sb(name, shape, dtype, tag=None):
            return held.tile(shape, dtype, name=name, tag=tag or name, align_bytes=64)

        def bank(index, shape):
            return psum.tile(shape, F32, name="bank%d" % index)

        lists = {}
        for name in ("c1", "offs", "c2", "mate"):
            lists[name] = held.tile([P, LIST_COLS], U16, name="list_" + name)

        x_plane = sb("x_plane", [P, T], U8)
        x_table = sb("x_table", [P, T], I32)
        raw_plane = {w: sb("raw_plane%d" % w, [P, H], U8) for w in (1, 2)}
        raw_plane[3] = placed.tile([P, H], U8, name="raw_plane3", offset=PAIR_BYTES - H // 2)
        raw_codes = {w: sb("raw_codes%d" % w, [P, 2 * H], U8) for w in (1, 2, 3)}
        gain = sb("gain", [P, PACK], F32)

        nc.vector.memset(x_plane[:].bitcast(I32), 0)
        for w in (2, 1, 3):
            nc.vector.memset(raw_plane[w][:].bitcast(I32), 0)

        def load_scale_rows(plane, rows, quads):
            for q in quads:
                nc.sync.dma_start(
                    out=plane[32 * q : 32 * q + 4, :].bitcast(I32), in_=rows[0, 4 * q : 4 * q + 4, :].bitcast(I32)
                )

        def load_codes(w, words):
            nc.sync.dma_start(out=raw_codes[w][:].bitcast(I32), in_=words[0].bitcast(I32))

        nc.sync.dma_start(lists["c1"][:], c1)
        nc.sync.dma_start(lists["offs"][:], offs)
        load_codes(2, w2_words)
        load_scale_rows(x_plane, x_scales, range(QUADS))
        nc.sync.dma_start(out=x_table[:], in_=x_words[0].rearrange("p n t -> p (n t)").bitcast(I32))
        load_scale_rows(raw_plane[2], w2_scales, range(QUADS))
        load_codes(1, w1_words)
        load_scale_rows(raw_plane[1], w1_scales, (0, 1))
        nc.sync.dma_start(lists["c2"][:], c2)
        load_scale_rows(raw_plane[1], w1_scales, (2, 3))
        nc.sync.dma_start(out=gain[:], in_=gn.rearrange("(p t) o -> p (t o)", t=PACK))
        nc.sync.dma_start(lists["mate"][:], mate)
        load_codes(3, w3_words)
        load_scale_rows(raw_plane[3], w3_scales, range(QUADS))

        codes = {w: sb("codes%d" % w, [P, 2 * H], U8) for w in (1, 2, 3)}
        plane = {w: sb("plane%d" % w, [P, H], U8) for w in (1, 2, 3)}

        def deal_codes(w, slots):
            nc.scalar.copy(
                out=codes[w][:].bitcast(U16).rearrange("p (t m) -> p t m", t=PACK)[:, slots],
                in_=raw_codes[w][:].bitcast(U16).rearrange("p (m t) -> p t m", t=PACK)[:, slots],
            )

        def deal_plane(w, slots):
            nc.gpsimd.tensor_copy(
                out=plane[w][:].rearrange("p (t m) -> p t m", t=PACK)[:, slots],
                in_=raw_plane[w][:].rearrange("p (m t) -> p t m", t=PACK)[:, slots],
            )

        warm_bf = sb("warm_bf", [P, PACK * P], BF16)
        warm_words = sb("warm_words", [P, P], U32)
        warm_scales = sb("warm_scales", [P, P], U8)
        nc.vector.tensor_copy(
            out=warm_bf[:].rearrange("p (a n) -> p a n", a=2),
            in_=raw_codes[2][:].bitcast(I32).unsqueeze(1).to_broadcast([P, 2, 2 * P]),
        )
        nc.vector.quantize_mx(out=warm_words[:].bitcast(FP8X4), scales=warm_scales[:], in_=warm_bf[:])

        for w in (2, 1):
            deal_codes(w, slice(0, PACK))
        for w, slots in ((2, slice(1, 4, 2)), (2, slice(0, 4, 2)), (1, slice(0, 4)), (3, slice(0, 4))):
            deal_plane(w, slots)
        nc.gpsimd.tensor_copy(
            out=codes[3][:].rearrange("p (t m b) -> p t m b", t=PACK, b=2),
            in_=raw_codes[3][:].rearrange("p (m t b) -> p t m b", t=PACK, b=2),
        )

        picked_scales = {}
        picked_words = {}

        def gather_scales(name):
            picked_scales[name] = sb("scales_" + name, [P, S], U8)
            nc.vector.tensor_copy(picked_scales[name][:], x_plane[:].indirect(lists[name][:]))

        def gather_words(name):
            picked_words[name] = sb("words_" + name, [P, S], U32)
            nc.vector.tensor_copy(picked_words[name][:], x_table[:].bitcast(U32).indirect(lists[name][:]))

        def gather_half(picked, name, table, h):
            nc.vector.tensor_copy(
                picked[name][:, h * HALF : (h + 1) * HALF],
                table.indirect(lists[name][:, h * HALF // 16 : (h + 1) * HALF // 16]),
            )

        def mx_pass(acc, w, t, words, scales, start, stop):
            nc.tensor.matmul_mx(
                out=acc,
                lhsT=codes[w][:, 2 * t * P : 2 * (t + 1) * P].bitcast(FP4X4),
                lhsT_scale=plane[w][:, t * P : (t + 1) * P],
                rhs=words.bitcast(FP8X4),
                rhs_scale=scales,
                start=start,
                stop=stop,
            )

        def first_layer_pass(acc, w, t, name, start):
            mx_pass(acc[:], w, t, picked_words[name][:], picked_scales[name][:], start, not start)

        gather_scales("c1")
        warm_acc = bank(7, [P, S])
        for n in range(2):
            nc.tensor.matmul_mx(
                out=warm_acc[:],
                lhsT=warm_words[:].bitcast(FP8X4),
                lhsT_scale=warm_scales[:],
                rhs=raw_codes[2][:].bitcast(FP4X4),
                rhs_scale=picked_scales["c1"][:],
                start=True,
                stop=True,
            )
        gather_scales("offs")
        picked_words["c1"] = sb("words_c1", [P, S], U32)
        for h in range(2):
            gather_half(picked_words, "c1", x_table[:].bitcast(U32), h)
        gather_words("offs")
        picked_scales["c2"] = sb("scales_c2", [P, S], U8)
        picked_words["c2"] = sb("words_c2", [P, S], U32)
        for h in range(2):
            gather_half(picked_scales, "c2", x_plane[:], h)
            gather_half(picked_words, "c2", x_table[:].bitcast(U32), h)

        gain_size = sb("gain_size", [P, PACK], F32)
        gain_sign = sb("gain_sign", [P, PACK], BF16)
        nc.scalar.activation(out=gain_size[:], in_=gain[:], func=ACT.Abs)
        nc.scalar.activation(out=gain_sign[:], in_=gain[:], func=ACT.Sign)

        order = (1, 3, 0, 2)
        y_acc = [bank(t, [P, S]) for t in range(PACK)]
        relu_y = [sb("relu_y%d" % t, [P, S], F32) for t in range(PACK)]
        for h in range(2):
            cols = slice(h * HALF, (h + 1) * HALF)
            for t in order:
                mx_pass(y_acc[t][:, cols], 2, t, picked_words["c1"][:, cols], picked_scales["c1"][:, cols], h == 0, False)
        for t in order:
            first_layer_pass(y_acc[t], 1, t, "offs", False)
            nc.scalar.activation(out=relu_y[t][:], in_=y_acc[t][:], func=ACT.Relu, scale=gain_size[:, t : t + 1])

        pair = [placed.tile([P, 2 * S], F32, name="pair%d" % u, offset=u * PAIR_BYTES) for u in range(2)]
        odd = [sb("odd%d" % u, [P, S], F32) for u in range(2)]
        window = [pair[0], odd[0], pair[1], odd[1]]
        halves = [slice(0, HALF), slice(HALF, S)]
        chunks = [slice(c * CHUNK, (c + 1) * CHUNK) for c in range(S // CHUNK)]

        for h in range(2):
            cols = halves[h]
            for group in range(2):
                slots = order[2 * group : 2 * group + 2]
                e_acc = bank(4 + 2 * h + group, [P, 2, HALF])
                for w, name in ((1, "c1"), (2, "c2")):
                    for i, t in enumerate(slots):
                        mx_pass(
                            e_acc[:, i, :], w, t, picked_words[name][:, cols], picked_scales[name][:, cols],
                            (w, i) == (1, 0), (w, i) == (2, 1),
                        )
                for i, t in enumerate(slots):
                    nc.vector.scalar_tensor_tensor(
                        out=window[t][:, cols], in0=e_acc[:, i, :], scalar=gain_size[:, t : t + 1],
                        in1=relu_y[t][:, cols], op0=ALU.mult, op1=ALU.max,
                    )
                    if h == 1 and t % 2:
                        nc.gpsimd.tensor_copy(out=pair[t // 2][:, S : 2 * S], in_=odd[t // 2][:])

        mates = [sb("mates0", [P, PACK, HALF], F32), sb("mates1", [P, PACK, HALF], F32, tag="relu_y2")]
        sums = [sb("sums%d" % h, [P, 2, 2 * HALF], BF16) for h in range(2)]
        z_bf = [sb("z_bf%d" % h, [P, PACK * HALF], BF16) for h in range(2)]
        z_words = [sb("z_words%d" % h, [P, HALF], U32) for h in range(2)]
        z_scales = [sb("z_scales%d" % h, [P, HALF], U8) for h in range(2)]

        def fetch_mates(t, h):
            entries = lists["mate"][:, h * HALF // 16 : (h + 1) * HALF // 16]
            if h == 0 and t % 2 == 0:
                nc.vector.tensor_copy(mates[h][:, t, :], window[t][:].indirect(entries))
            else:
                nc.scalar.activation(out=mates[h][:, t, :], in_=window[t][:].indirect(entries), func=ACT.Copy)

        def add_mates(u, h, cols):
            own = pair[u][:].rearrange("p (e j) -> p e j", e=2)[:, :, h * HALF + cols.start : h * HALF + cols.stop]
            nc.vector.tensor_tensor(
                out=sums[h][:, u, 2 * cols.start : 2 * cols.stop].rearrange("p (c i e) -> p c e i", i=4, e=2),
                in0=own.rearrange("p e (c i) -> p c e i", i=4),
                in1=mates[h][:, 2 * u : 2 * u + 2, cols].rearrange("p e (c i) -> p c e i", i=4),
                op=ALU.add,
            )

        def sign_z(h, cols):
            width = cols.stop - cols.start
            nc.vector.tensor_tensor(
                out=z_bf[h][:, PACK * cols.start : PACK * cols.stop].rearrange("p (j u e) -> p j u e", u=2, e=2),
                in0=sums[h][:, :, 2 * cols.start : 2 * cols.stop].rearrange("p u (j e) -> p j u e", e=2),
                in1=gain_sign[:].rearrange("p (u e) -> p u e", e=2).unsqueeze(1).to_broadcast([P, width, 2, 2]),
                op=ALU.mult,
            )

        def quantise_z(h, cols):
            nc.vector.quantize_mx(
                out=z_words[h][:, cols].bitcast(FP8X4),
                scales=z_scales[h][:, cols],
                in_=z_bf[h][:, PACK * cols.start : PACK * cols.stop],
            )

        for t in order:
            fetch_mates(t, 0)
        for t in (1, 0, 3, 2):
            fetch_mates(t, 1)
        add_mates(0, 0, chunks[0])
        add_mates(1, 0, chunks[0])
        add_mates(0, 0, chunks[1])
        sign_z(0, chunks[0])
        add_mates(1, 0, chunks[1])
        quantise_z(0, chunks[0])
        sign_z(0, chunks[1])
        add_mates(0, 1, halves[0])
        quantise_z(0, chunks[1])
        for cols in chunks[:2]:
            add_mates(1, 1, cols)
        for step in (sign_z, quantise_z):
            for cols in chunks[:2]:
                step(1, cols)

        out_rows = out_0.rearrange("(p t) j -> p t j", t=PACK)
        out_words = out_1[0].rearrange("p n t -> p (n t)").bitcast(I32)
        y_scales = sb("y_scales", [P, S], U8)
        y_words = sb("y_words", [P, S], U32)
        result_bf = sb("result_bf", [P, PACK * S], BF16, tag="z_bf1")

        def hand_on(cols):
            wide = slice(PACK * cols.start, PACK * cols.stop)
            nc.vector.quantize_mx(out=y_words[:, cols].bitcast(FP8X4), scales=y_scales[:, cols], in_=result_bf[:, wide])

        first = sb("first", [P, 2, PACK, CHUNK], F32)
        result = [first[:, 0], first[:, 1]] + [sb("result%d" % c, [P, PACK, CHUNK], F32)[:] for c in (2, 3)]

        def second_product(acc, c, slots):
            for i, t in enumerate(slots):
                mx_pass(acc[:, i, :], 3, t, z_words[c // 2][:, chunks[c % 2]], z_scales[c // 2][:, chunks[c % 2]], True, True)

        def round_result(c):
            dst, src = interleaved(result_bf[:, c * PACK * CHUNK : (c + 1) * PACK * CHUNK], result[c])
            nc.vector.tensor_copy(out=dst, in_=src)

        for c in range(3):
            acc = bank(c, [P, PACK, CHUNK])
            second_product(acc, c, range(PACK))
            nc.scalar.copy(out=result[c], in_=acc[:])
            nc.sync.dma_start(out=out_rows[:, :, chunks[c]], in_=result[c])
        nc.vector.tensor_copy(
            out=result_bf[:, 0 : PACK * HALF].rearrange("p (b c i t) -> p b c t i", b=2, i=4, t=PACK),
            in_=first[:].rearrange("p b t (c i) -> p b c t i", i=4),
        )
        for duo, copy in enumerate((nc.vector.tensor_copy, nc.scalar.copy)):
            acc = bank(3 + duo, [P, 2, CHUNK])
            second_product(acc, 3, (2 * duo, 2 * duo + 1))
            copy(out=result[3][:, 2 * duo : 2 * duo + 2, :], in_=acc[:])
        nc.sync.dma_start(out=out_rows[:, :, chunks[3]], in_=result[3])
        hand_on(halves[0])
        nc.sync.dma_start(out=out_words[:, halves[0]], in_=y_words[:, halves[0]].bitcast(I32))
        for c in (2, 3):
            round_result(c)
        for c in (2, 3):
            hand_on(chunks[c])
        nc.sync.dma_start(out=out_words[:, halves[1]], in_=y_words[:, halves[1]].bitcast(I32))
        for q in range(QUADS):
            queue = nc.scalar if q % 2 else nc.sync
            queue.dma_start(out=out_2[0, 4 * q : 4 * q + 4, :].bitcast(I32), in_=y_scales[32 * q : 32 * q + 4, :].bitcast(I32))
